import numpy as np
import ml_dtypes


def mxq(x, axis, fmt="e4m3"):
    dtype, down = {"e4m3": (ml_dtypes.float8_e4m3fn, 7), "e5m2": (ml_dtypes.float8_e5m2, 14)}[fmt]
    v = np.moveaxis(np.asarray(x, np.float32).astype(ml_dtypes.bfloat16).astype(np.float64), axis, -1)
    blocks = v.reshape(v.shape[:-1] + (-1, 32))
    amax = np.abs(blocks).max(-1, keepdims=True)
    byte = np.maximum(np.where(amax > 0, np.frexp(amax)[1] - 1 + 127, 0) - down, 1)
    scale = np.exp2(byte - 127.0)
    codes = (blocks / scale).astype(np.float32).astype(dtype).astype(np.float64)
    return np.moveaxis((codes * scale).reshape(v.shape), -1, axis)


WIDE = False


def mx_kscale(k):
    if not WIDE:
        return np.ones(k)
    levels = np.array([18, -18])
    if k % 512:
        return np.exp2(np.random.permutation(np.resize(levels, k // 32))).repeat(32)
    a = np.empty((k // 512, 16))
    for p in range(k // 512):
        a[p, :8] = np.random.permutation(np.resize(levels, 8))
        for g in range(8):
            far = levels[np.abs(levels - a[p, g]) >= 10]
            a[p, g + 8] = far[np.random.randint(len(far))]
    return np.exp2(a.ravel()).repeat(32)


def f64(x):
    return np.asarray(x).astype(np.float64)


def striped(idx):
    return np.tile(np.asarray(idx).reshape(-1, 16).T, (8, 1)).astype(np.uint16)


def unstriped(offs):
    return offs[:16].T.reshape(-1).astype(np.int64)

def planes(y):
    n, m = y.shape
    v = y.astype(np.float32).astype(ml_dtypes.bfloat16).astype(np.float64).reshape(n // 32, 32, m)
    top = np.abs(v).max(1)
    byte = np.clip(np.where(top > 0, np.frexp(top)[1] - 1 + 127 - 7, 1), 1, 254)
    codes = (v * np.exp2(127.0 - byte)[:, None, :]).reshape(n, m).astype(np.float32).astype(ml_dtypes.float8_e4m3fn).view(np.uint8)
    words = codes.reshape(n // 512, 128, 4, m).transpose(0, 1, 3, 2)
    return np.ascontiguousarray(words), np.ascontiguousarray(byte.astype(np.uint8).reshape(n // 512, 16, m))


T, C, D, DV = 1024, 512, 512, 512
BETA = 0.25


def setup_inputs():
    n = np.random.standard_normal
    grid = lambda v: np.clip(np.round(v * 16) / 16, -4, 4)
    v = mx_kscale(DV)[:, None]
    return {
        "zT": (grid(n((DV, T))) * v).astype(np.float32),
        "cb": (grid(n((DV, C))) * v).astype(np.float32),
        "wm": (n((DV, D)) / np.sqrt(DV) / v).astype(np.float32),
        "offs": striped(np.random.randint(0, C, T)),
    }


def reference(zT, cb, wm, offs):
    e = f64(zT) - f64(cb)[:, unstriped(offs)]
    g = BETA * e
    out_0 = mxq(f64(wm), 0, "e4m3").T @ mxq(g, 0, "e5m2")
    return (out_0,) + planes(out_0)

@@ -1,0 +1,189 @@
+from contextlib import ExitStack
+
+import concourse.mybir as mybir
+
+T, C, D, DV = 1024, 512, 512, 512
+BETA = 0.25
+FLOPS = 2 * T * D * DV
+
+F32 = mybir.dt.float32
+BF16 = mybir.dt.bfloat16
+I32 = mybir.dt.int32
+U32 = mybir.dt.uint32
+U16 = mybir.dt.uint16
+U8 = mybir.dt.uint8
+E4M3 = mybir.dt.float8_e4m3fn_x4
+E5M2 = mybir.dt.float8_e5m2_x4
+COPY = mybir.ActivationFunctionType.Copy
+SUB = mybir.AluOpType.subtract
+MULT = mybir.AluOpType.mult
+
+P = 128
+LANES = 4
+HALF = 512
+QUARTER = 256
+RUN = 4
+
+
+def weave(src, dst):
+    return (dst.rearrange("p (c i) l -> p c l i", i=RUN), src.rearrange("p l (c i) -> p c l i", i=RUN))
+
+
+def tile_attend_gvq_pl_c_x_kernel(tc, zT, cb, wm, offs, out_0, out_1, out_2):
+    nc = tc.nc
+    with ExitStack() as ctx:
+        sb = ctx.enter_context(tc.tile_pool(name="sb", bufs=1))
+        ps = ctx.enter_context(tc.psum_pool(name="ps", bufs=1))
+
+        offsets = sb.tile([P, T // 16], U16, name="offsets")
+        book = [sb.tile([P, C], F32, name="book%d" % l) for l in range(LANES)]
+        za = [sb.tile([P, HALF], F32, name="za%d" % l) for l in range(2)]
+        zb = [sb.tile([P, 2, QUARTER], F32, name="zb%d" % q) for q in range(2)]
+        z = [None, None] + [sb.tile([P, LANES, QUARTER], F32, name="z%d" % q) for q in range(2, 4)]
+        w_raw = [sb.tile([P, LANES, D // 2], F32, name="w_raw%d" % u) for u in range(2)]
+        diff = [sb.tile([P, LANES, QUARTER], F32, name="diff%d" % q) for q in range(3)]
+        g_bf = [sb.tile([P, HALF, LANES], BF16, name="g_bf%d" % h, align_bytes=64) for h in range(2)]
+        g_codes = [sb.tile([P, HALF], U32, name="g_codes%d" % h, align_bytes=64) for h in range(2)]
+        g_scales = [sb.tile([P, HALF], U8, name="g_scales%d" % h, align_bytes=64) for h in range(2)]
+        w_bf = sb.tile([P, LANES, P, LANES], BF16, name="w_bf", tag="w_bf", align_bytes=64)
+        w_codes = sb.tile([P, D], U32, name="w_codes", align_bytes=64)
+        w_scales = sb.tile([P, D], U8, name="w_scales", align_bytes=64)
+        y = [sb.tile([P, LANES, HALF], F32, name="y%d" % h) for h in range(2)]
+        y_bf = [sb.tile([P, HALF, LANES], BF16, name="y_bf%d" % h, align_bytes=64) for h in range(2)]
+        y_codes = sb.tile([P, T], U32, name="y_codes", align_bytes=64)
+        y_scales = sb.tile([P, T], U8, name="y_scales", align_bytes=64)
+        acc = [[ps.tile([P, HALF], F32, name="acc%d_%d" % (h, l)) for l in range(LANES)] for h in range(2)]
+
+        cb_v = cb.rearrange("(p l) c -> p l c", l=LANES)
+        z_v = zT.rearrange("(p l) t -> p l t", l=LANES)
+        w_v = wm.rearrange("(p l) d -> p l d", l=LANES)
+        out_v = out_0.rearrange("(p l) t -> p l t", l=LANES)
+        words_v = out_1[0].rearrange("p t l -> p (t l)").bitcast(I32)
+        scales_v = out_2[0].bitcast(I32)
+
+        def load_z(q):
+            nc.sync.dma_start(out=z[q][:], in_=z_v[:, :, q * QUARTER:(q + 1) * QUARTER])
+
+        def load_w(u):
+            nc.sync.dma_start(out=w_raw[u][:], in_=w_v[:, :, u * 256:(u + 1) * 256])
+
+        def z_of(q, l):
+            if q >= 2:
+                return z[q][:, l, :]
+            if l < 2:
+                return za[l][:, q * QUARTER:(q + 1) * QUARTER]
+            return zb[q][:, l - 2, :]
+
+        def gather(q, l):
+            nc.vector.tensor_tensor(diff[q][:, l, :], book[l][:].indirect(offsets[:, 16 * q:16 * (q + 1)]), z_of(q, l), SUB)
+
+        def round_g(a, b, on_vector):
+            q, h = a // QUARTER, a // HALF
+            dst, src = weave(diff[q][:, :, a - q * QUARTER:b - q * QUARTER], g_bf[h][:, a - h * HALF:b - h * HALF, :])
+            if on_vector:
+                nc.vector.tensor_scalar(dst, src, -BETA, None, MULT)
+            else:
+                nc.scalar.activation(dst, src, COPY, scale=-BETA)
+
+        def quant_g(a, b):
+            h = a // HALF
+            cols = slice(a - h * HALF, b - h * HALF)
+            nc.vector.quantize_mx(out=g_codes[h][:, cols].bitcast(E5M2), scales=g_scales[h][:, cols],
+                                  in_=g_bf[h][:, cols, :].rearrange("p t l -> p (t l)"))
+
+        def round_w(u):
+            nc.scalar.activation(w_bf[:, :, 64 * u:64 * (u + 1), :].rearrange("p j m l -> p m l j"),
+                                 w_raw[u][:].rearrange("p l (m j) -> p m l j", j=LANES), COPY)
+
+        def quant_w():
+            nc.vector.quantize_mx(out=w_codes[:].bitcast(E4M3), scales=w_scales[:],
+                                  in_=w_bf[:].rearrange("p j m l -> p (j m l)"))
+
+        def multiply(h, j):
+            cols = slice(j * P, (j + 1) * P)
+            nc.tensor.matmul_mx(out=acc[h][j][:], lhsT=w_codes[:, cols].bitcast(E4M3), lhsT_scale=w_scales[:, cols],
+                                rhs=g_codes[h][:].bitcast(E5M2), rhs_scale=g_scales[h][:], start=True, stop=True)
+
+        def drain(h, j, on_vector):
+            if on_vector:
+                nc.vector.tensor_copy(y[h][:, j, :], acc[h][j][:])
+            else:
+                nc.scalar.activation(y[h][:, j, :], acc[h][j][:], COPY)
+            nc.sync.dma_start(out=out_v[:, j, h * HALF:(h + 1) * HALF], in_=y[h][:, j, :])
+
+        def round_y(a, b, on_vector):
+            h = a // HALF
+            cols = slice(a - h * HALF, b - h * HALF)
+            dst, src = weave(y[h][:, :, cols], y_bf[h][:, cols, :])
+            if on_vector:
+                nc.vector.tensor_copy(dst, src)
+            else:
+                nc.scalar.activation(dst, src, COPY)
+
+        def quant_y(a, b):
+            h = a // HALF
+            nc.vector.quantize_mx(out=y_codes[:, a:b].bitcast(E4M3), scales=y_scales[:, a:b],
+                                  in_=y_bf[h][:, a - h * HALF:b - h * HALF, :].rearrange("p t l -> p (t l)"))
+
+        def load_book(l):
+            nc.sync.dma_start(out=book[l][:], in_=cb_v[:, l, :])
+
+        def store_codes(a, b):
+            nc.sync.dma_start(out=words_v[:, a:b], in_=y_codes[:, a:b].bitcast(I32))
+
+        def store_scales():
+            for k in range(4):
+                eng = nc.sync if k % 2 == 0 else nc.scalar
+                eng.dma_start(out=scales_v[4 * k:4 * k + 4, :], in_=y_scales[32 * k:32 * k + 4, :].bitcast(I32))
+
+        nc.sync.dma_start(offsets[:], offs)
+        for l in range(2):
+            load_book(l)
+            nc.sync.dma_start(out=za[l][:], in_=z_v[:, l, 0:HALF])
+        for q in range(2):
+            load_book(2 + q)
+            nc.sync.dma_start(out=zb[q][:], in_=z_v[:, 2:4, q * QUARTER:(q + 1) * QUARTER])
+        load_w(0)
+        load_z(2)
+        load_w(1)
+        load_z(3)
+
+        for l in range(2):
+            gather(0, l)
+            gather(1, l)
+        for q in range(2):
+            gather(q, 2)
+            gather(q, 3)
+        round_g(0, 256, False)
+        round_w(0)
+        round_g(256, 512, False)
+        round_w(1)
+        for l in range(LANES):
+            gather(2, l)
+        quant_g(0, 512)
+        quant_w()
+        round_g(512, 768, False)
+        for j in range(LANES):
+            multiply(0, j)
+            drain(0, j, False)
+        diff.append(sb.tile([P, LANES, QUARTER], F32, name="diff3", tag="w_bf", align_bytes=64))
+        for l in range(LANES):
+            gather(3, l)
+        quant_g(512, 768)
+        round_g(768, 1024, True)
+        quant_g(768, 1024)
+        round_y(0, 384, False)
+        round_y(384, 512, True)
+        for j in range(LANES):
+            multiply(1, j)
+        for j in range(LANES):
+            drain(1, j, j % 2 == 0)
+        quant_y(0, 512)
+        store_codes(0, HALF)
+        round_y(512, 768, True)
+        round_y(768, 896, False)
+        round_y(896, 1024, True)
+        quant_y(512, 768)
+        quant_y(768, 1024)
+        store_codes(HALF, T)
+        store_scales()

@@ -37,11 +37,10 @@ def tile_attend_gvq_pl_c_x_kernel(tc, zT, cb, wm, offs, out_0, out_1, out_2):
 
         offsets = sb.tile([P, T // 16], U16, name="offsets")
         book = [sb.tile([P, C], F32, name="book%d" % l) for l in range(LANES)]
-        za = [sb.tile([P, HALF], F32, name="za%d" % l) for l in range(2)]
-        zb = [sb.tile([P, 2, QUARTER], F32, name="zb%d" % q) for q in range(2)]
-        z = [None, None] + [sb.tile([P, LANES, QUARTER], F32, name="z%d" % q) for q in range(2, 4)]
-        w_raw = [sb.tile([P, LANES, D // 2], F32, name="w_raw%d" % u) for u in range(2)]
-        diff = [sb.tile([P, LANES, QUARTER], F32, name="diff%d" % q) for q in range(3)]
+        z = [[sb.tile([P, HALF], F32, name="z%d_%d" % (h, l)) for l in range(LANES)] for h in range(2)]
+        w_raw = sb.tile([P, LANES, D], F32, name="w_raw")
+        spans = [(0, 256), (256, 512), (512, 896), (896, 1024)]
+        diff = [sb.tile([P, LANES, b - a], F32, name="diff%d" % a) for a, b in spans[:3]]
         g_bf = [sb.tile([P, HALF, LANES], BF16, name="g_bf%d" % h, align_bytes=64) for h in range(2)]
         g_codes = [sb.tile([P, HALF], U32, name="g_codes%d" % h, align_bytes=64) for h in range(2)]
         g_scales = [sb.tile([P, HALF], U8, name="g_scales%d" % h, align_bytes=64) for h in range(2)]
@@ -61,25 +60,21 @@ def tile_attend_gvq_pl_c_x_kernel(tc, zT, cb, wm, offs, out_0, out_1, out_2):
         words_v = out_1[0].rearrange("p t l -> p (t l)").bitcast(I32)
         scales_v = out_2[0].bitcast(I32)
 
-        def load_z(q):
-            nc.sync.dma_start(out=z[q][:], in_=z_v[:, :, q * QUARTER:(q + 1) * QUARTER])
+        def load_z(h, l):
+            nc.sync.dma_start(out=z[h][l][:], in_=z_v[:, l, h * HALF:(h + 1) * HALF])
 
-        def load_w(u):
-            nc.sync.dma_start(out=w_raw[u][:], in_=w_v[:, :, u * 256:(u + 1) * 256])
+        def diff_of(a, b):
+            k = [i for i, s in enumerate(spans) if s[0] <= a < s[1]][0]
+            return diff[k][:, :, a - spans[k][0]:b - spans[k][0]]
 
-        def z_of(q, l):
-            if q >= 2:
-                return z[q][:, l, :]
-            if l < 2:
-                return za[l][:, q * QUARTER:(q + 1) * QUARTER]
-            return zb[q][:, l - 2, :]
-
-        def gather(q, l):
-            nc.vector.tensor_tensor(diff[q][:, l, :], book[l][:].indirect(offsets[:, 16 * q:16 * (q + 1)]), z_of(q, l), SUB)
+        def gather(a, b, l):
+            h = a // HALF
+            nc.vector.tensor_tensor(diff_of(a, b)[:, l, :], book[l][:].indirect(offsets[:, a // 16:b // 16]),
+                                    z[h][l][:, a - h * HALF:b - h * HALF], SUB)
 
         def round_g(a, b, on_vector):
-            q, h = a // QUARTER, a // HALF
-            dst, src = weave(diff[q][:, :, a - q * QUARTER:b - q * QUARTER], g_bf[h][:, a - h * HALF:b - h * HALF, :])
+            h = a // HALF
+            dst, src = weave(diff_of(a, b), g_bf[h][:, a - h * HALF:b - h * HALF, :])
             if on_vector:
                 nc.vector.tensor_scalar(dst, src, -BETA, None, MULT)
             else:
@@ -91,9 +86,9 @@ def tile_attend_gvq_pl_c_x_kernel(tc, zT, cb, wm, offs, out_0, out_1, out_2):
             nc.vector.quantize_mx(out=g_codes[h][:, cols].bitcast(E5M2), scales=g_scales[h][:, cols],
                                   in_=g_bf[h][:, cols, :].rearrange("p t l -> p (t l)"))
 
-        def round_w(u):
-            nc.scalar.activation(w_bf[:, :, 64 * u:64 * (u + 1), :].rearrange("p j m l -> p m l j"),
-                                 w_raw[u][:].rearrange("p l (m j) -> p m l j", j=LANES), COPY)
+        def round_w():
+            nc.scalar.activation(w_bf[:].rearrange("p j m l -> p m l j"),
+                                 w_raw[:].rearrange("p l (m j) -> p m l j", j=LANES), COPY)
 
         def quant_w():
             nc.vector.quantize_mx(out=w_codes[:].bitcast(E4M3), scales=w_scales[:],
@@ -137,52 +132,51 @@ def tile_attend_gvq_pl_c_x_kernel(tc, zT, cb, wm, offs, out_0, out_1, out_2):
                 eng.dma_start(out=scales_v[4 * k:4 * k + 4, :], in_=y_scales[32 * k:32 * k + 4, :].bitcast(I32))
 
         nc.sync.dma_start(offsets[:], offs)
-        for l in range(2):
-            load_book(l)
-            nc.sync.dma_start(out=za[l][:], in_=z_v[:, l, 0:HALF])
-        for q in range(2):
-            load_book(2 + q)
-            nc.sync.dma_start(out=zb[q][:], in_=z_v[:, 2:4, q * QUARTER:(q + 1) * QUARTER])
-        load_w(0)
-        load_z(2)
-        load_w(1)
-        load_z(3)
-
-        for l in range(2):
-            gather(0, l)
-            gather(1, l)
-        for q in range(2):
-            gather(q, 2)
-            gather(q, 3)
-        round_g(0, 256, False)
-        round_w(0)
-        round_g(256, 512, False)
-        round_w(1)
         for l in range(LANES):
-            gather(2, l)
+            load_book(l)
+            load_z(0, l)
+        load_z(1, 0)
+        load_z(1, 1)
+        nc.sync.dma_start(out=w_raw[:], in_=w_v)
+        load_z(1, 2)
+        load_z(1, 3)
+
+        for l in range(LANES):
+            gather(0, 256, l)
+            gather(256, 512, l)
+        round_g(0, 256, False)
+        round_g(256, 512, False)
+        round_w()
+        for l in range(2):
+            gather(512, 768, l)
+            gather(768, 896, l)
         quant_g(0, 512)
+        for l in range(2, 4):
+            gather(512, 768, l)
+            gather(768, 896, l)
         quant_w()
+        diff.append(sb.tile([P, LANES, 128], F32, name="diff_last", tag="w_bf", align_bytes=64))
+        for l in range(LANES):
+            gather(896, 1024, l)
         round_g(512, 768, False)
+        round_g(768, 896, False)
         for j in range(LANES):
             multiply(0, j)
             drain(0, j, False)
-        diff.append(sb.tile([P, LANES, QUARTER], F32, name="diff3", tag="w_bf", align_bytes=64))
-        for l in range(LANES):
-            gather(3, l)
+        round_g(896, 1024, True)
         quant_g(512, 768)
-        round_g(768, 1024, True)
         quant_g(768, 1024)
-        round_y(0, 384, False)
-        round_y(384, 512, True)
         for j in range(LANES):
             multiply(1, j)
-        for j in range(LANES):
-            drain(1, j, j % 2 == 0)
+        round_y(0, 512, True)
+        for j in range(3):
+            drain(1, j, False)
         quant_y(0, 512)
         store_codes(0, HALF)
+        drain(1, 3, True)
         round_y(512, 768, True)
-        round_y(768, 896, False)
-        round_y(896, 1024, True)
+        round_y(768, 960, False)
+        round_y(960, 1024, True)
         quant_y(512, 768)
         quant_y(768, 1024)
         store_codes(HALF, T)

@@ -36,14 +36,15 @@ def tile_attend_gvq_pl_c_x_kernel(tc, zT, cb, wm, offs, out_0, out_1, out_2):
         ps = ctx.enter_context(tc.psum_pool(name="ps", bufs=1))
 
         offsets = sb.tile([P, T // 16], U16, name="offsets")
-        book = [sb.tile([P, C], F32, name="book%d" % l) for l in range(LANES)]
+        book = [sb.tile([P, 2 * C if l < 3 else C], F32, name="book%d" % l) for l in range(LANES)]
         z = [[sb.tile([P, HALF], F32, name="z%d_%d" % (h, l)) for l in range(LANES)] for h in range(2)]
-        w_raw = sb.tile([P, LANES, D], F32, name="w_raw")
-        spans = [(0, 256), (256, 512), (512, 896), (896, 1024)]
-        diff = [sb.tile([P, LANES, b - a], F32, name="diff%d" % a) for a, b in spans[:3]]
-        g_bf = [sb.tile([P, HALF, LANES], BF16, name="g_bf%d" % h, align_bytes=64) for h in range(2)]
-        g_codes = [sb.tile([P, HALF], U32, name="g_codes%d" % h, align_bytes=64) for h in range(2)]
-        g_scales = [sb.tile([P, HALF], U8, name="g_scales%d" % h, align_bytes=64) for h in range(2)]
+        w_raw = sb.tile([P, LANES, D], F32, name="w_raw", tag="w_raw", align_bytes=64)
+        spans = [(0, 512), (512, 896), (896, 1024)]
+        diff = [sb.tile([P, LANES, b - a], F32, name="diff%d" % a) for a, b in spans[:2]]
+        g_spans = [(0, 512), (512, 768), (768, 1024)]
+        g_bf = [sb.tile([P, b - a, LANES], BF16, name="g_bf%d" % a, align_bytes=64) for a, b in g_spans[:2]]
+        g_codes = sb.tile([P, T], U32, name="g_codes", align_bytes=64)
+        g_scales = sb.tile([P, T], U8, name="g_scales", align_bytes=64)
         w_bf = sb.tile([P, LANES, P, LANES], BF16, name="w_bf", tag="w_bf", align_bytes=64)
         w_codes = sb.tile([P, D], U32, name="w_codes", align_bytes=64)
         w_scales = sb.tile([P, D], U8, name="w_scales", align_bytes=64)
@@ -51,7 +52,6 @@ def tile_attend_gvq_pl_c_x_kernel(tc, zT, cb, wm, offs, out_0, out_1, out_2):
         y_bf = [sb.tile([P, HALF, LANES], BF16, name="y_bf%d" % h, align_bytes=64) for h in range(2)]
         y_codes = sb.tile([P, T], U32, name="y_codes", align_bytes=64)
         y_scales = sb.tile([P, T], U8, name="y_scales", align_bytes=64)
-        acc = [[ps.tile([P, HALF], F32, name="acc%d_%d" % (h, l)) for l in range(LANES)] for h in range(2)]
 
         cb_v = cb.rearrange("(p l) c -> p l c", l=LANES)
         z_v = zT.rearrange("(p l) t -> p l t", l=LANES)
@@ -67,44 +67,50 @@ def tile_attend_gvq_pl_c_x_kernel(tc, zT, cb, wm, offs, out_0, out_1, out_2):
             k = [i for i, s in enumerate(spans) if s[0] <= a < s[1]][0]
             return diff[k][:, :, a - spans[k][0]:b - spans[k][0]]
 
+        def g_of(a, b):
+            k = [i for i, s in enumerate(g_spans) if s[0] <= a < s[1]][0]
+            return g_bf[k][:, a - g_spans[k][0]:b - g_spans[k][0], :]
+
         def gather(a, b, l):
             h = a // HALF
             nc.vector.tensor_tensor(diff_of(a, b)[:, l, :], book[l][:].indirect(offsets[:, a // 16:b // 16]),
                                     z[h][l][:, a - h * HALF:b - h * HALF], SUB)
 
         def round_g(a, b, on_vector):
-            h = a // HALF
-            dst, src = weave(diff_of(a, b), g_bf[h][:, a - h * HALF:b - h * HALF, :])
+            dst, src = weave(diff_of(a, b), g_of(a, b))
             if on_vector:
                 nc.vector.tensor_scalar(dst, src, -BETA, None, MULT)
             else:
                 nc.scalar.activation(dst, src, COPY, scale=-BETA)
 
         def quant_g(a, b):
-            h = a // HALF
-            cols = slice(a - h * HALF, b - h * HALF)
-            nc.vector.quantize_mx(out=g_codes[h][:, cols].bitcast(E5M2), scales=g_scales[h][:, cols],
-                                  in_=g_bf[h][:, cols, :].rearrange("p t l -> p (t l)"))
+            nc.vector.quantize_mx(out=g_codes[:, a:b].bitcast(E5M2), scales=g_scales[:, a:b],
+                                  in_=g_of(a, b).rearrange("p t l -> p (t l)"))
 
         def round_w():
             nc.scalar.activation(w_bf[:].rearrange("p j m l -> p m l j"),
                                  w_raw[:].rearrange("p l (m j) -> p m l j", j=LANES), COPY)
 
-        def quant_w():
-            nc.vector.quantize_mx(out=w_codes[:].bitcast(E4M3), scales=w_scales[:],
-                                  in_=w_bf[:].rearrange("p j m l -> p (j m l)"))
+        def quant_w(j0, j1):
+            cols = slice(j0 * P, j1 * P)
+            nc.vector.quantize_mx(out=w_codes[:, cols].bitcast(E4M3), scales=w_scales[:, cols],
+                                  in_=w_bf[:, j0:j1, :, :].rearrange("p j m l -> p (j m l)"))
 
-        def multiply(h, j):
+        def multiply(j, a, bank):
             cols = slice(j * P, (j + 1) * P)
-            nc.tensor.matmul_mx(out=acc[h][j][:], lhsT=w_codes[:, cols].bitcast(E4M3), lhsT_scale=w_scales[:, cols],
-                                rhs=g_codes[h][:].bitcast(E5M2), rhs_scale=g_scales[h][:], start=True, stop=True)
+            acc = ps.tile([P, HALF], F32, name="acc%d_%d" % (j, a), tag="bank%d" % bank)
+            nc.tensor.matmul_mx(out=acc[:], lhsT=w_codes[:, cols].bitcast(E4M3), lhsT_scale=w_scales[:, cols],
+                                rhs=g_codes[:, a:a + HALF].bitcast(E5M2), rhs_scale=g_scales[:, a:a + HALF],
+                                start=True, stop=True)
+            return acc
 
-        def drain(h, j, on_vector):
-            if on_vector:
-                nc.vector.tensor_copy(y[h][:, j, :], acc[h][j][:])
-            else:
-                nc.scalar.activation(y[h][:, j, :], acc[h][j][:], COPY)
-            nc.sync.dma_start(out=out_v[:, j, h * HALF:(h + 1) * HALF], in_=y[h][:, j, :])
+        def drain(acc, first, j, a, b):
+            h = a // HALF
+            nc.scalar.activation(y[h][:, j, a - h * HALF:b - h * HALF], acc[:, a - first:b - first], COPY)
+
+        def store_y(j0, j1, a, b):
+            h = a // HALF
+            nc.sync.dma_start(out=out_v[:, j0:j1, a:b], in_=y[h][:, j0:j1, a - h * HALF:b - h * HALF])
 
         def round_y(a, b, on_vector):
             h = a // HALF
@@ -121,7 +127,7 @@ def tile_attend_gvq_pl_c_x_kernel(tc, zT, cb, wm, offs, out_0, out_1, out_2):
                                   in_=y_bf[h][:, a - h * HALF:b - h * HALF, :].rearrange("p t l -> p (t l)"))
 
         def load_book(l):
-            nc.sync.dma_start(out=book[l][:], in_=cb_v[:, l, :])
+            nc.sync.dma_start(out=book[l][:, 0:C], in_=cb_v[:, l, :])
 
         def store_codes(a, b):
             nc.sync.dma_start(out=words_v[:, a:b], in_=y_codes[:, a:b].bitcast(I32))
@@ -140,43 +146,57 @@ def tile_attend_gvq_pl_c_x_kernel(tc, zT, cb, wm, offs, out_0, out_1, out_2):
         nc.sync.dma_start(out=w_raw[:], in_=w_v)
         load_z(1, 2)
         load_z(1, 3)
+        for l in range(3):
+            nc.vector.memset(book[l][:, C:2 * C], 0.0)
 
-        for l in range(LANES):
-            gather(0, 256, l)
-            gather(256, 512, l)
+        for l in range(3):
+            gather(0, 512, l)
+        gather(0, 256, 3)
+        gather(256, 512, 3)
         round_g(0, 256, False)
         round_g(256, 512, False)
         round_w()
         for l in range(2):
-            gather(512, 768, l)
-            gather(768, 896, l)
+            gather(512, 896, l)
         quant_g(0, 512)
-        for l in range(2, 4):
-            gather(512, 768, l)
-            gather(768, 896, l)
-        quant_w()
+        gather(512, 896, 2)
+        gather(512, 768, 3)
+        gather(768, 896, 3)
+        quant_w(0, 2)
+        quant_w(2, 4)
+        g_bf.append(sb.tile([P, 256, LANES], BF16, name="g_tail", tag="w_raw", align_bytes=64))
+        round_g(768, 896, True)
         diff.append(sb.tile([P, LANES, 128], F32, name="diff_last", tag="w_bf", align_bytes=64))
         for l in range(LANES):
             gather(896, 1024, l)
         round_g(512, 768, False)
-        round_g(768, 896, False)
         for j in range(LANES):
-            multiply(0, j)
-            drain(0, j, False)
-        round_g(896, 1024, True)
+            drain(multiply(j, 0, j), 0, j, 0, 512)
+            store_y(j, j + 1, 0, 512)
         quant_g(512, 768)
-        quant_g(768, 1024)
-        for j in range(LANES):
-            multiply(1, j)
-        round_y(0, 512, True)
-        for j in range(3):
-            drain(1, j, False)
-        quant_y(0, 512)
+        quant_g(768, 896)
+        early = [multiply(j, 384, 4 + j) for j in range(2)]
+        round_g(896, 1024, True)
+        quant_g(896, 1024)
+        for j in range(2):
+            drain(early[j], 384, j, 512, 896)
+        store_y(0, 2, 512, 896)
+        late = {j: multiply(j, 512, bank) for j, bank in ((2, 6), (3, 7), (0, 0), (1, 1))}
+        round_y(0, 256, True)
+        round_y(256, 512, True)
+        drain(late[2], 512, 2, 512, 1024)
+        store_y(2, 3, 512, 1024)
+        quant_y(0, 256)
+        quant_y(256, 512)
         store_codes(0, HALF)
-        drain(1, 3, True)
+        drain(late[3], 512, 3, 512, 1024)
+        store_y(3, 4, 512, 1024)
+        for j in range(2):
+            drain(late[j], 512, j, 896, 1024)
+        store_y(0, 2, 896, 1024)
         round_y(512, 768, True)
-        round_y(768, 960, False)
-        round_y(960, 1024, True)
+        round_y(768, 928, False)
+        round_y(928, 1024, True)
         quant_y(512, 768)
         quant_y(768, 1024)
         store_codes(HALF, T)

@@ -23,6 +23,10 @@ LANES = 4
 HALF = 512
 QUARTER = 256
 RUN = 4
+WV = 16
+MID = 736
+YS = 96
+YE = 928
 
 
 def weave(src, dst):
@@ -36,16 +40,22 @@ def tile_attend_gvq_pl_c_x_kernel(tc, zT, cb, wm, offs, out_0, out_1, out_2):
         ps = ctx.enter_context(tc.psum_pool(name="ps", bufs=1))
 
         offsets = sb.tile([P, T // 16], U16, name="offsets")
-        book = [sb.tile([P, 2 * C if l < 3 else C], F32, name="book%d" % l) for l in range(LANES)]
-        z = [[sb.tile([P, HALF], F32, name="z%d_%d" % (h, l)) for l in range(LANES)] for h in range(2)]
-        w_raw = sb.tile([P, LANES, D], F32, name="w_raw", tag="w_raw", align_bytes=64)
-        spans = [(0, 512), (512, 896), (896, 1024)]
-        diff = [sb.tile([P, LANES, b - a], F32, name="diff%d" % a) for a, b in spans[:2]]
-        g_spans = [(0, 512), (512, 768), (768, 1024)]
-        g_bf = [sb.tile([P, b - a, LANES], BF16, name="g_bf%d" % a, align_bytes=64) for a, b in g_spans[:2]]
+        book = [sb.tile([P, 2 * C if l < 3 else C], F32, name="book%d" % l, tag="book%d" % l, align_bytes=64) for l in range(LANES)]
+        z = [{} for l in range(LANES)]
+
+        raw = sb.tile([P, 240 + LANES * D], F32, name="raw", align_bytes=64)
+        rounded = sb.tile([P, 2032], F32, name="rounded", align_bytes=64)
+        diff = {0: sb.tile([P, LANES, 512], F32, name="diff0")[:],
+                512: sb.tile([P, LANES, MID - 512], F32, name="diff512")[:],
+                MID: rounded[:, 0:LANES * (896 - MID)].rearrange("p (l t) -> p l t", l=LANES),
+                896: raw[:, 0:512].rearrange("p (l t) -> p l t", l=LANES)}
+        g_bf = {0: sb.tile([P, 512, LANES], BF16, name="g_bf0", align_bytes=64)[:],
+                512: rounded[:, 768:1536].bitcast(BF16).rearrange("p (t l) -> p t l", l=LANES),
+                896: sb.tile([P, 128, LANES], BF16, name="g_bf896", align_bytes=64)[:]}
         g_codes = sb.tile([P, T], U32, name="g_codes", align_bytes=64)
         g_scales = sb.tile([P, T], U8, name="g_scales", align_bytes=64)
-        w_bf = sb.tile([P, LANES, P, LANES], BF16, name="w_bf", tag="w_bf", align_bytes=64)
+        w_bf = [rounded[:, a:a + 512].bitcast(BF16).rearrange("p (j m l) -> p j m l", j=2, l=LANES) for a in (272, 1520)]
+        w_raw = raw[:, 240:].rearrange("p (l d) -> p l d", l=LANES)
         w_codes = sb.tile([P, D], U32, name="w_codes", align_bytes=64)
         w_scales = sb.tile([P, D], U8, name="w_scales", align_bytes=64)
         y = [sb.tile([P, LANES, HALF], F32, name="y%d" % h) for h in range(2)]
@@ -60,41 +70,56 @@ def tile_attend_gvq_pl_c_x_kernel(tc, zT, cb, wm, offs, out_0, out_1, out_2):
         words_v = out_1[0].rearrange("p t l -> p (t l)").bitcast(I32)
         scales_v = out_2[0].bitcast(I32)
 
-        def load_z(h, l):
-            nc.sync.dma_start(out=z[h][l][:], in_=z_v[:, l, h * HALF:(h + 1) * HALF])
+        def within(tiles, a, b):
+            first = max(s for s in tiles if s <= a)
+            return tiles[first], slice(a - first, b - first)
 
-        def diff_of(a, b):
-            k = [i for i, s in enumerate(spans) if s[0] <= a < s[1]][0]
-            return diff[k][:, :, a - spans[k][0]:b - spans[k][0]]
+        def load_book(l):
+            nc.sync.dma_start(out=book[l][:, 0:C], in_=cb_v[:, l, :])
 
-        def g_of(a, b):
-            k = [i for i, s in enumerate(g_spans) if s[0] <= a < s[1]][0]
-            return g_bf[k][:, a - g_spans[k][0]:b - g_spans[k][0], :]
+        def load_z_lane(l, a, b):
+            tile = sb.tile([P, b - a], F32, name="z%d_%d" % (a, l))
+            nc.sync.dma_start(out=tile[:], in_=z_v[:, l, a:b])
+            z[l][a] = tile[:]
+
+        def load_z(l0, l1, a, b):
+            tile = sb.tile([P, l1 - l0, b - a], F32, name="z%d_%d_%d" % (a, l0, l1))
+            nc.sync.dma_start(out=tile[:], in_=z_v[:, l0:l1, a:b])
+            for l in range(l0, l1):
+                z[l][a] = tile[:, l - l0, :]
 
         def gather(a, b, l):
-            h = a // HALF
-            nc.vector.tensor_tensor(diff_of(a, b)[:, l, :], book[l][:].indirect(offsets[:, a // 16:b // 16]),
-                                    z[h][l][:, a - h * HALF:b - h * HALF], SUB)
+            src, zc = within(z[l], a, b)
+            dst, dc = within(diff, a, b)
+            nc.vector.tensor_tensor(dst[:, l, dc], book[l][:].indirect(offsets[:, a // 16:b // 16]), src[:, zc], SUB)
 
         def round_g(a, b, on_vector):
-            dst, src = weave(diff_of(a, b), g_of(a, b))
+            src, sc = within(diff, a, b)
+            dst, dc = within(g_bf, a, b)
+            dst, src = weave(src[:, :, sc], dst[:, dc, :])
             if on_vector:
                 nc.vector.tensor_scalar(dst, src, -BETA, None, MULT)
             else:
                 nc.scalar.activation(dst, src, COPY, scale=-BETA)
 
         def quant_g(a, b):
+            src, sc = within(g_bf, a, b)
             nc.vector.quantize_mx(out=g_codes[:, a:b].bitcast(E5M2), scales=g_scales[:, a:b],
-                                  in_=g_of(a, b).rearrange("p t l -> p (t l)"))
+                                  in_=src[:, sc, :].rearrange("p t l -> p (t l)"))
 
-        def round_w():
-            nc.scalar.activation(w_bf[:].rearrange("p j m l -> p m l j"),
-                                 w_raw[:].rearrange("p l (m j) -> p m l j", j=LANES), COPY)
+        def round_w(q, m0, m1, on_vector):
+            dst = w_bf[q][:, :, m0:m1, :].rearrange("p j m l -> p m l j")
+            src = w_raw.rearrange("p l (m j) -> p m l j", j=LANES)[:, m0:m1, :, 2 * q:2 * q + 2]
+            if on_vector:
+                nc.vector.tensor_copy(dst, src)
+            else:
+                nc.scalar.activation(dst, src, COPY)
 
         def quant_w(j0, j1):
             cols = slice(j0 * P, j1 * P)
+            src = w_bf[j0 // 2][:, j0 % 2:j0 % 2 + j1 - j0, :, :]
             nc.vector.quantize_mx(out=w_codes[:, cols].bitcast(E4M3), scales=w_scales[:, cols],
-                                  in_=w_bf[:, j0:j1, :, :].rearrange("p j m l -> p (j m l)"))
+                                  in_=src.rearrange("p j m l -> p (j m l)"))
 
         def multiply(j, a, bank):
             cols = slice(j * P, (j + 1) * P)
@@ -104,9 +129,13 @@ def tile_attend_gvq_pl_c_x_kernel(tc, zT, cb, wm, offs, out_0, out_1, out_2):
                                 start=True, stop=True)
             return acc
 
-        def drain(acc, first, j, a, b):
+        def drain(acc, first, j, a, b, on_vector=False):
             h = a // HALF
-            nc.scalar.activation(y[h][:, j, a - h * HALF:b - h * HALF], acc[:, a - first:b - first], COPY)
+            dst, src = y[h][:, j, a - h * HALF:b - h * HALF], acc[:, a - first:b - first]
+            if on_vector:
+                nc.vector.tensor_copy(dst, src)
+            else:
+                nc.scalar.activation(dst, src, COPY)
 
         def store_y(j0, j1, a, b):
             h = a // HALF
@@ -126,9 +155,6 @@ def tile_attend_gvq_pl_c_x_kernel(tc, zT, cb, wm, offs, out_0, out_1, out_2):
             nc.vector.quantize_mx(out=y_codes[:, a:b].bitcast(E4M3), scales=y_scales[:, a:b],
                                   in_=y_bf[h][:, a - h * HALF:b - h * HALF, :].rearrange("p t l -> p (t l)"))
 
-        def load_book(l):
-            nc.sync.dma_start(out=book[l][:, 0:C], in_=cb_v[:, l, :])
-
         def store_codes(a, b):
             nc.sync.dma_start(out=words_v[:, a:b], in_=y_codes[:, a:b].bitcast(I32))
 
@@ -140,63 +166,65 @@ def tile_attend_gvq_pl_c_x_kernel(tc, zT, cb, wm, offs, out_0, out_1, out_2):
         nc.sync.dma_start(offsets[:], offs)
         for l in range(LANES):
             load_book(l)
-            load_z(0, l)
-        load_z(1, 0)
-        load_z(1, 1)
-        nc.sync.dma_start(out=w_raw[:], in_=w_v)
-        load_z(1, 2)
-        load_z(1, 3)
+            load_z_lane(l, 0, 512)
+        load_z(0, LANES, 512, MID)
+        nc.sync.dma_start(out=w_raw, in_=w_v)
+        load_z(0, 1, MID, T)
+        load_z(1, LANES, MID, T)
         for l in range(3):
             nc.vector.memset(book[l][:, C:2 * C], 0.0)
 
         for l in range(3):
             gather(0, 512, l)
-        gather(0, 256, 3)
-        gather(256, 512, 3)
-        round_g(0, 256, False)
-        round_g(256, 512, False)
-        round_w()
-        for l in range(2):
-            gather(512, 896, l)
-        quant_g(0, 512)
-        gather(512, 896, 2)
-        gather(512, 768, 3)
-        gather(768, 896, 3)
-        quant_w(0, 2)
-        quant_w(2, 4)
-        g_bf.append(sb.tile([P, 256, LANES], BF16, name="g_tail", tag="w_raw", align_bytes=64))
-        round_g(768, 896, True)
-        diff.append(sb.tile([P, LANES, 128], F32, name="diff_last", tag="w_bf", align_bytes=64))
+        for a, b in ((0, 256), (256, 512)):
+            gather(a, b, 3)
+            round_g(a, b, False)
         for l in range(LANES):
-            gather(896, 1024, l)
-        round_g(512, 768, False)
-        for j in range(LANES):
-            drain(multiply(j, 0, j), 0, j, 0, 512)
-            store_y(j, j + 1, 0, 512)
+            gather(512, MID, l)
+        round_w(0, WV, 128, False)
+        round_w(1, 0, 128, False)
+        quant_g(0, 512)
+        round_w(0, 0, WV, True)
+        gather(MID, 896, 0)
+        gather(896, T, 0)
+        quant_w(0, 1)
+        quant_w(1, 2)
+        for l in range(1, LANES):
+            gather(MID, 896, l)
+        quant_w(2, 4)
+        round_g(512, MID, False)
+        first = [multiply(j, 0, j) for j in range(LANES)]
+        gather(896, T, 1)
+        round_g(MID, 896, True)
+        gather(896, T, 2)
         quant_g(512, 768)
         quant_g(768, 896)
         early = [multiply(j, 384, 4 + j) for j in range(2)]
+        gather(896, T, 3)
         round_g(896, 1024, True)
         quant_g(896, 1024)
+        for j in range(4):
+            drain(first[j], 0, j, 0, 512)
+            store_y(j, j + 1, 0, 512)
         for j in range(2):
             drain(early[j], 384, j, 512, 896)
         store_y(0, 2, 512, 896)
-        late = {j: multiply(j, 512, bank) for j, bank in ((2, 6), (3, 7), (0, 0), (1, 1))}
-        round_y(0, 256, True)
-        round_y(256, 512, True)
-        drain(late[2], 512, 2, 512, 1024)
+        last = {j: multiply(j, 512, bank) for j, bank in ((2, 6), (3, 7), (0, 0), (1, 1))}
+        round_y(0, YS, False)
+        round_y(YS, 512, True)
+        quant_y(0, 512)
+        drain(last[2], 512, 2, 512, 1024)
         store_y(2, 3, 512, 1024)
-        quant_y(0, 256)
-        quant_y(256, 512)
         store_codes(0, HALF)
-        drain(late[3], 512, 3, 512, 1024)
+        drain(last[3], 512, 3, 512, 768)
+        drain(last[3], 512, 3, 768, 1024)
         store_y(3, 4, 512, 1024)
         for j in range(2):
-            drain(late[j], 512, j, 896, 1024)
+            drain(last[j], 512, j, 896, 1024, False)
         store_y(0, 2, 896, 1024)
         round_y(512, 768, True)
-        round_y(768, 928, False)
-        round_y(928, 1024, True)
+        round_y(768, YE, True)
+        round_y(YE, 1024, False)
         quant_y(512, 768)
         quant_y(768, 1024)
         store_codes(HALF, T)

@@ -23,10 +23,9 @@ LANES = 4
 HALF = 512
 QUARTER = 256
 RUN = 4
-WV = 16
-MID = 736
+WV = 48
 YS = 96
-YE = 928
+YE = 896
 
 
 def weave(src, dst):
@@ -43,19 +42,17 @@ def tile_attend_gvq_pl_c_x_kernel(tc, zT, cb, wm, offs, out_0, out_1, out_2):
         book = [sb.tile([P, 2 * C if l < 3 else C], F32, name="book%d" % l, tag="book%d" % l, align_bytes=64) for l in range(LANES)]
         z = [{} for l in range(LANES)]
 
-        raw = sb.tile([P, 240 + LANES * D], F32, name="raw", align_bytes=64)
-        rounded = sb.tile([P, 2032], F32, name="rounded", align_bytes=64)
+        late = sb.tile([P, LANES * 2304], F32, name="late", align_bytes=64)
         diff = {0: sb.tile([P, LANES, 512], F32, name="diff0")[:],
-                512: sb.tile([P, LANES, MID - 512], F32, name="diff512")[:],
-                MID: rounded[:, 0:LANES * (896 - MID)].rearrange("p (l t) -> p l t", l=LANES),
-                896: raw[:, 0:512].rearrange("p (l t) -> p l t", l=LANES)}
+                512: late[:, 7024:8048].rearrange("p (l t) -> p l t", l=LANES),
+                768: late[:].rearrange("p (l t) -> p l t", l=LANES)[:, :, 0:256]}
         g_bf = {0: sb.tile([P, 512, LANES], BF16, name="g_bf0", align_bytes=64)[:],
-                512: rounded[:, 768:1536].bitcast(BF16).rearrange("p (t l) -> p t l", l=LANES),
-                896: sb.tile([P, 128, LANES], BF16, name="g_bf896", align_bytes=64)[:]}
+                768: sb.tile([P, 256, LANES], BF16, name="g_bf768", align_bytes=64)[:]}
         g_codes = sb.tile([P, T], U32, name="g_codes", align_bytes=64)
         g_scales = sb.tile([P, T], U8, name="g_scales", align_bytes=64)
-        w_bf = [rounded[:, a:a + 512].bitcast(BF16).rearrange("p (j m l) -> p j m l", j=2, l=LANES) for a in (272, 1520)]
-        w_raw = raw[:, 240:].rearrange("p (l d) -> p l d", l=LANES)
+        w_bf = [late[:, 2544:3056].bitcast(BF16).rearrange("p (j m l) -> p j m l", j=2, l=LANES),
+                sb.tile([P, 2, P, LANES], BF16, name="w_bf1", align_bytes=64)[:]]
+        w_raw = late[:, 4848:6896].rearrange("p (l d) -> p l d", l=LANES)
         w_codes = sb.tile([P, D], U32, name="w_codes", align_bytes=64)
         w_scales = sb.tile([P, D], U8, name="w_scales", align_bytes=64)
         y = [sb.tile([P, LANES, HALF], F32, name="y%d" % h) for h in range(2)]
@@ -83,7 +80,7 @@ def tile_attend_gvq_pl_c_x_kernel(tc, zT, cb, wm, offs, out_0, out_1, out_2):
             z[l][a] = tile[:]
 
         def load_z(l0, l1, a, b):
-            tile = sb.tile([P, l1 - l0, b - a], F32, name="z%d_%d_%d" % (a, l0, l1))
+            tile = sb.tile([P, l1 - l0, b - a], F32, name="z%d_%d_%d" % (a, l0, l1), align_bytes=64)
             nc.sync.dma_start(out=tile[:], in_=z_v[:, l0:l1, a:b])
             for l in range(l0, l1):
                 z[l][a] = tile[:, l - l0, :]
@@ -167,10 +164,10 @@ def tile_attend_gvq_pl_c_x_kernel(tc, zT, cb, wm, offs, out_0, out_1, out_2):
         for l in range(LANES):
             load_book(l)
             load_z_lane(l, 0, 512)
-        load_z(0, LANES, 512, MID)
+        load_z(0, LANES, 512, 768)
         nc.sync.dma_start(out=w_raw, in_=w_v)
-        load_z(0, 1, MID, T)
-        load_z(1, LANES, MID, T)
+        load_z(0, 1, 768, T)
+        load_z(1, LANES, 768, T)
         for l in range(3):
             nc.vector.memset(book[l][:, C:2 * C], 0.0)
 
@@ -180,35 +177,34 @@ def tile_attend_gvq_pl_c_x_kernel(tc, zT, cb, wm, offs, out_0, out_1, out_2):
             gather(a, b, 3)
             round_g(a, b, False)
         for l in range(LANES):
-            gather(512, MID, l)
+            gather(512, 768, l)
         round_w(0, WV, 128, False)
         round_w(1, 0, 128, False)
         quant_g(0, 512)
         round_w(0, 0, WV, True)
-        gather(MID, 896, 0)
-        gather(896, T, 0)
+        gather(768, T, 0)
         quant_w(0, 1)
         quant_w(1, 2)
-        for l in range(1, LANES):
-            gather(MID, 896, l)
+        gather(768, T, 1)
         quant_w(2, 4)
-        round_g(512, MID, False)
+        gather(768, T, 2)
+        g_bf[512] = sb.tile([P, 256, LANES], BF16, name="g_bf512", tag="z768_0_1", align_bytes=64)[:]
+        round_g(512, 768, False)
         first = [multiply(j, 0, j) for j in range(LANES)]
-        gather(896, T, 1)
-        round_g(MID, 896, True)
-        gather(896, T, 2)
         quant_g(512, 768)
-        quant_g(768, 896)
-        early = [multiply(j, 384, 4 + j) for j in range(2)]
+        early = [multiply(j, 256, 4 + j) for j in range(2)]
+        gather(768, 896, 3)
         gather(896, T, 3)
-        round_g(896, 1024, True)
-        quant_g(896, 1024)
+        round_g(768, 896, True)
+        round_g(896, T, True)
+        quant_g(768, 896)
+        quant_g(896, T)
         for j in range(4):
             drain(first[j], 0, j, 0, 512)
             store_y(j, j + 1, 0, 512)
         for j in range(2):
-            drain(early[j], 384, j, 512, 896)
-        store_y(0, 2, 512, 896)
+            drain(early[j], 256, j, 512, 768)
+        store_y(0, 2, 512, 768)
         last = {j: multiply(j, 512, bank) for j, bank in ((2, 6), (3, 7), (0, 0), (1, 1))}
         round_y(0, YS, False)
         round_y(YS, 512, True)
@@ -220,8 +216,8 @@ def tile_attend_gvq_pl_c_x_kernel(tc, zT, cb, wm, offs, out_0, out_1, out_2):
         drain(last[3], 512, 3, 768, 1024)
         store_y(3, 4, 512, 1024)
         for j in range(2):
-            drain(last[j], 512, j, 896, 1024, False)
-        store_y(0, 2, 896, 1024)
+            drain(last[j], 512, j, 768, 1024, False)
+        store_y(0, 2, 768, 1024)
         round_y(512, 768, True)
         round_y(768, YE, True)
         round_y(YE, 1024, False)

@@ -23,9 +23,7 @@ LANES = 4
 HALF = 512
 QUARTER = 256
 RUN = 4
-WV = 48
-YS = 96
-YE = 896
+YE = 864
 
 
 def weave(src, dst):
@@ -41,18 +39,15 @@ def tile_attend_gvq_pl_c_x_kernel(tc, zT, cb, wm, offs, out_0, out_1, out_2):
         offsets = sb.tile([P, T // 16], U16, name="offsets")
         book = [sb.tile([P, 2 * C if l < 3 else C], F32, name="book%d" % l, tag="book%d" % l, align_bytes=64) for l in range(LANES)]
         z = [{} for l in range(LANES)]
-
-        late = sb.tile([P, LANES * 2304], F32, name="late", align_bytes=64)
-        diff = {0: sb.tile([P, LANES, 512], F32, name="diff0")[:],
-                512: late[:, 7024:8048].rearrange("p (l t) -> p l t", l=LANES),
-                768: late[:].rearrange("p (l t) -> p l t", l=LANES)[:, :, 0:256]}
-        g_bf = {0: sb.tile([P, 512, LANES], BF16, name="g_bf0", align_bytes=64)[:],
-                768: sb.tile([P, 256, LANES], BF16, name="g_bf768", align_bytes=64)[:]}
+        late = sb.tile([P, 752 + LANES * D], F32, name="late", align_bytes=64)
+        w_raw = late[:, 752:].rearrange("p (l d) -> p l d", l=LANES)
+        diff = {0: sb.tile([P, LANES, 512], F32, name="diff0"),
+                512: sb.tile([P, LANES, 256], F32, name="diff512", tag="diff512"),
+                768: late[:, 0:1024].rearrange("p (l t) -> p l t", l=LANES)}
+        g_bf = {a: sb.tile([P, n, LANES], BF16, name="g_bf%d" % a, align_bytes=64) for a, n in ((0, 512), (768, 256))}
         g_codes = sb.tile([P, T], U32, name="g_codes", align_bytes=64)
         g_scales = sb.tile([P, T], U8, name="g_scales", align_bytes=64)
-        w_bf = [late[:, 2544:3056].bitcast(BF16).rearrange("p (j m l) -> p j m l", j=2, l=LANES),
-                sb.tile([P, 2, P, LANES], BF16, name="w_bf1", align_bytes=64)[:]]
-        w_raw = late[:, 4848:6896].rearrange("p (l d) -> p l d", l=LANES)
+        w_bf = [sb.tile([P, 2, P, LANES], BF16, name="w_bf%d" % q, align_bytes=64)[:] for q in range(2)]
         w_codes = sb.tile([P, D], U32, name="w_codes", align_bytes=64)
         w_scales = sb.tile([P, D], U8, name="w_scales", align_bytes=64)
         y = [sb.tile([P, LANES, HALF], F32, name="y%d" % h) for h in range(2)]
@@ -178,50 +173,54 @@ def tile_attend_gvq_pl_c_x_kernel(tc, zT, cb, wm, offs, out_0, out_1, out_2):
             round_g(a, b, False)
         for l in range(LANES):
             gather(512, 768, l)
-        round_w(0, WV, 128, False)
+        round_w(0, 0, 128, False)
         round_w(1, 0, 128, False)
         quant_g(0, 512)
-        round_w(0, 0, WV, True)
         gather(768, T, 0)
-        quant_w(0, 1)
-        quant_w(1, 2)
+        quant_w(0, 2)
         gather(768, T, 1)
+        gather(768, 896, 2)
         quant_w(2, 4)
-        gather(768, T, 2)
-        g_bf[512] = sb.tile([P, 256, LANES], BF16, name="g_bf512", tag="z768_0_1", align_bytes=64)[:]
+        gather(896, T, 2)
+        g_bf[512] = sb.tile([P, 256, LANES], BF16, name="g_bf512", tag="z768_0_1", align_bytes=64)
         round_g(512, 768, False)
         first = [multiply(j, 0, j) for j in range(LANES)]
-        quant_g(512, 768)
-        early = [multiply(j, 256, 4 + j) for j in range(2)]
         gather(768, 896, 3)
         gather(896, T, 3)
+        quant_g(512, 768)
+        early = [multiply(j, 256, 4 + j) for j in range(2)]
         round_g(768, 896, True)
         round_g(896, T, True)
         quant_g(768, 896)
         quant_g(896, T)
-        for j in range(4):
+        for j in range(2):
             drain(first[j], 0, j, 0, 512)
+            store_y(j, j + 1, 0, 512)
+        for j in range(2, 4):
+            drain(first[j], 0, j, 0, 256)
+        for j in range(2, 4):
+            drain(first[j], 0, j, 256, 512)
             store_y(j, j + 1, 0, 512)
         for j in range(2):
             drain(early[j], 256, j, 512, 768)
         store_y(0, 2, 512, 768)
         last = {j: multiply(j, 512, bank) for j, bank in ((2, 6), (3, 7), (0, 0), (1, 1))}
-        round_y(0, YS, False)
-        round_y(YS, 512, True)
-        quant_y(0, 512)
-        drain(last[2], 512, 2, 512, 1024)
-        store_y(2, 3, 512, 1024)
+        round_y(0, 256, True)
+        round_y(256, 512, True)
+        quant_y(0, 256)
+        quant_y(256, 512)
+        drain(last[2], 512, 2, 512, T)
+        store_y(2, 3, 512, T)
         store_codes(0, HALF)
         drain(last[3], 512, 3, 512, 768)
-        drain(last[3], 512, 3, 768, 1024)
-        store_y(3, 4, 512, 1024)
+        drain(last[3], 512, 3, 768, T)
+        store_y(3, 4, 512, T)
         for j in range(2):
             drain(last[j], 512, j, 768, 1024, False)
         store_y(0, 2, 768, 1024)
         round_y(512, 768, True)
-        round_y(768, YE, True)
-        round_y(YE, 1024, False)
-        quant_y(512, 768)
-        quant_y(768, 1024)
+        round_y(768, YE, False)
+        round_y(YE, 1024, True)
+        quant_y(512, T)
         store_codes(HALF, T)
         store_scales()

@@ -23,7 +23,8 @@ LANES = 4
 HALF = 512
 QUARTER = 256
 RUN = 4
-YE = 864
+YM = 608
+YE = 832
 
 
 def weave(src, dst):
@@ -39,12 +40,13 @@ def tile_attend_gvq_pl_c_x_kernel(tc, zT, cb, wm, offs, out_0, out_1, out_2):
         offsets = sb.tile([P, T // 16], U16, name="offsets")
         book = [sb.tile([P, 2 * C if l < 3 else C], F32, name="book%d" % l, tag="book%d" % l, align_bytes=64) for l in range(LANES)]
         z = [{} for l in range(LANES)]
-        late = sb.tile([P, 752 + LANES * D], F32, name="late", align_bytes=64)
-        w_raw = late[:, 752:].rearrange("p (l d) -> p l d", l=LANES)
+        late = sb.tile([P, 1008 + LANES * D + 496], F32, name="late", align_bytes=64)
+        w_raw = late[:, 1008:3056].rearrange("p (l d) -> p l d", l=LANES)
         diff = {0: sb.tile([P, LANES, 512], F32, name="diff0"),
                 512: sb.tile([P, LANES, 256], F32, name="diff512", tag="diff512"),
                 768: late[:, 0:1024].rearrange("p (l t) -> p l t", l=LANES)}
-        g_bf = {a: sb.tile([P, n, LANES], BF16, name="g_bf%d" % a, align_bytes=64) for a, n in ((0, 512), (768, 256))}
+        g_bf = {a: sb.tile([P, n, LANES], BF16, name="g_bf%d" % a, align_bytes=64) for a, n in ((0, 512),)}
+        g_bf[768] = late[:, 3040:3552].bitcast(BF16).rearrange("p (t l) -> p t l", l=LANES)
         g_codes = sb.tile([P, T], U32, name="g_codes", align_bytes=64)
         g_scales = sb.tile([P, T], U8, name="g_scales", align_bytes=64)
         w_bf = [sb.tile([P, 2, P, LANES], BF16, name="w_bf%d" % q, align_bytes=64)[:] for q in range(2)]
@@ -179,28 +181,25 @@ def tile_attend_gvq_pl_c_x_kernel(tc, zT, cb, wm, offs, out_0, out_1, out_2):
         gather(768, T, 0)
         quant_w(0, 2)
         gather(768, T, 1)
-        gather(768, 896, 2)
-        quant_w(2, 4)
-        gather(896, T, 2)
+        gather(768, T, 2)
+        gather(768, 896, 3)
+        quant_w(2, 3)
+        quant_w(3, 4)
         g_bf[512] = sb.tile([P, 256, LANES], BF16, name="g_bf512", tag="z768_0_1", align_bytes=64)
         round_g(512, 768, False)
         first = [multiply(j, 0, j) for j in range(LANES)]
-        gather(768, 896, 3)
         gather(896, T, 3)
-        quant_g(512, 768)
-        early = [multiply(j, 256, 4 + j) for j in range(2)]
         round_g(768, 896, True)
         round_g(896, T, True)
-        quant_g(768, 896)
-        quant_g(896, T)
-        for j in range(2):
+        quant_g(512, 768)
+        early = [multiply(j, 256, 4 + j) for j in range(2)]
+        quant_g(768, T)
+        for j in range(3):
             drain(first[j], 0, j, 0, 512)
             store_y(j, j + 1, 0, 512)
-        for j in range(2, 4):
-            drain(first[j], 0, j, 0, 256)
-        for j in range(2, 4):
-            drain(first[j], 0, j, 256, 512)
-            store_y(j, j + 1, 0, 512)
+        drain(first[3], 0, 3, 0, 256)
+        drain(first[3], 0, 3, 256, 512)
+        store_y(3, 4, 0, 512)
         for j in range(2):
             drain(early[j], 256, j, 512, 768)
         store_y(0, 2, 512, 768)
@@ -218,9 +217,11 @@ def tile_attend_gvq_pl_c_x_kernel(tc, zT, cb, wm, offs, out_0, out_1, out_2):
         for j in range(2):
             drain(last[j], 512, j, 768, 1024, False)
         store_y(0, 2, 768, 1024)
-        round_y(512, 768, True)
+        round_y(YM, 768, True)
+        round_y(512, YM, False)
         round_y(768, YE, False)
-        round_y(YE, 1024, True)
-        quant_y(512, T)
+        round_y(YE, T, True)
+        quant_y(512, 768)
+        quant_y(768, T)
         store_codes(HALF, T)
         store_scales()

@@ -168,6 +168,7 @@ def tile_attend_gvq_pl_c_x_kernel(tc, zT, cb, wm, offs, out_0, out_1, out_2):
         for l in range(3):
             nc.vector.memset(book[l][:, C:2 * C], 0.0)
 
+        nc.vector.tensor_copy(diff[768][:, 0, :], book[0][:].indirect(offsets[:, 48:64]))
         for l in range(3):
             gather(0, 512, l)
         for a, b in ((0, 256), (256, 512)):
@@ -178,7 +179,7 @@ def tile_attend_gvq_pl_c_x_kernel(tc, zT, cb, wm, offs, out_0, out_1, out_2):
         round_w(0, 0, 128, False)
         round_w(1, 0, 128, False)
         quant_g(0, 512)
-        gather(768, T, 0)
+        nc.vector.tensor_tensor(diff[768][:, 0, :], diff[768][:, 0, :], z[0][768], SUB)
         quant_w(0, 2)
         gather(768, T, 1)
         gather(768, T, 2)

@@ -20,11 +20,11 @@ MULT = mybir.AluOpType.mult
 
 P = 128
 LANES = 4
-HALF = 512
-QUARTER = 256
+Q1, HALF, Q3 = 256, 512, 768
 RUN = 4
-YM = 608
-YE = 832
+OVERLAP = 16
+Y3_SPLIT = 608
+Y4_SPLIT = 832
 
 
 def weave(src, dst):
@@ -38,18 +38,21 @@ def tile_attend_gvq_pl_c_x_kernel(tc, zT, cb, wm, offs, out_0, out_1, out_2):
         ps = ctx.enter_context(tc.psum_pool(name="ps", bufs=1))
 
         offsets = sb.tile([P, T // 16], U16, name="offsets")
-        book = [sb.tile([P, 2 * C if l < 3 else C], F32, name="book%d" % l, tag="book%d" % l, align_bytes=64) for l in range(LANES)]
+        book = [sb.tile([P, 2 * C if l < 3 else C], F32, name="book%d" % l, tag="book%d" % l, align_bytes=64)
+                for l in range(LANES)]
         z = [{} for l in range(LANES)]
-        late = sb.tile([P, 1008 + LANES * D + 496], F32, name="late", align_bytes=64)
-        w_raw = late[:, 1008:3056].rearrange("p (l d) -> p l d", l=LANES)
-        diff = {0: sb.tile([P, LANES, 512], F32, name="diff0"),
-                512: sb.tile([P, LANES, 256], F32, name="diff512", tag="diff512"),
-                768: late[:, 0:1024].rearrange("p (l t) -> p l t", l=LANES)}
-        g_bf = {a: sb.tile([P, n, LANES], BF16, name="g_bf%d" % a, align_bytes=64) for a, n in ((0, 512),)}
-        g_bf[768] = late[:, 3040:3552].bitcast(BF16).rearrange("p (t l) -> p t l", l=LANES)
+        w_at = LANES * (T - Q3) - OVERLAP
+        g_at = w_at + LANES * D - OVERLAP
+        late = sb.tile([P, g_at + LANES * (T - Q3) // 2], F32, name="late", align_bytes=64)
+        w_raw = late[:, w_at:w_at + LANES * D].rearrange("p (l d) -> p l d", l=LANES)
+        diff = {0: sb.tile([P, LANES, HALF], F32, name="diff0"),
+                HALF: sb.tile([P, LANES, Q3 - HALF], F32, name="diff512", tag="diff512"),
+                Q3: late[:, 0:LANES * (T - Q3)].rearrange("p (l t) -> p l t", l=LANES)}
+        g_bf = {0: sb.tile([P, HALF, LANES], BF16, name="g_bf0", align_bytes=64),
+                Q3: late[:, g_at:].bitcast(BF16).rearrange("p (t l) -> p t l", l=LANES)}
         g_codes = sb.tile([P, T], U32, name="g_codes", align_bytes=64)
         g_scales = sb.tile([P, T], U8, name="g_scales", align_bytes=64)
-        w_bf = [sb.tile([P, 2, P, LANES], BF16, name="w_bf%d" % q, align_bytes=64)[:] for q in range(2)]
+        w_bf = [sb.tile([P, 2, P, LANES], BF16, name="w_bf%d" % pair, align_bytes=64)[:] for pair in range(2)]
         w_codes = sb.tile([P, D], U32, name="w_codes", align_bytes=64)
         w_scales = sb.tile([P, D], U8, name="w_scales", align_bytes=64)
         y = [sb.tile([P, LANES, HALF], F32, name="y%d" % h) for h in range(2)]
@@ -65,11 +68,8 @@ def tile_attend_gvq_pl_c_x_kernel(tc, zT, cb, wm, offs, out_0, out_1, out_2):
         scales_v = out_2[0].bitcast(I32)
 
         def within(tiles, a, b):
-            first = max(s for s in tiles if s <= a)
-            return tiles[first], slice(a - first, b - first)
-
-        def load_book(l):
-            nc.sync.dma_start(out=book[l][:, 0:C], in_=cb_v[:, l, :])
+            start = max(s for s in tiles if s <= a)
+            return tiles[start], slice(a - start, b - start)
 
         def load_z_lane(l, a, b):
             tile = sb.tile([P, b - a], F32, name="z%d_%d" % (a, l))
@@ -82,10 +82,13 @@ def tile_attend_gvq_pl_c_x_kernel(tc, zT, cb, wm, offs, out_0, out_1, out_2):
             for l in range(l0, l1):
                 z[l][a] = tile[:, l - l0, :]
 
+        def codewords(a, b, l):
+            return book[l][:].indirect(offsets[:, a // 16:b // 16])
+
         def gather(a, b, l):
             src, zc = within(z[l], a, b)
             dst, dc = within(diff, a, b)
-            nc.vector.tensor_tensor(dst[:, l, dc], book[l][:].indirect(offsets[:, a // 16:b // 16]), src[:, zc], SUB)
+            nc.vector.tensor_tensor(dst[:, l, dc], codewords(a, b, l), src[:, zc], SUB)
 
         def round_g(a, b, on_vector):
             src, sc = within(diff, a, b)
@@ -101,13 +104,10 @@ def tile_attend_gvq_pl_c_x_kernel(tc, zT, cb, wm, offs, out_0, out_1, out_2):
             nc.vector.quantize_mx(out=g_codes[:, a:b].bitcast(E5M2), scales=g_scales[:, a:b],
                                   in_=src[:, sc, :].rearrange("p t l -> p (t l)"))
 
-        def round_w(q, m0, m1, on_vector):
-            dst = w_bf[q][:, :, m0:m1, :].rearrange("p j m l -> p m l j")
-            src = w_raw.rearrange("p l (m j) -> p m l j", j=LANES)[:, m0:m1, :, 2 * q:2 * q + 2]
-            if on_vector:
-                nc.vector.tensor_copy(dst, src)
-            else:
-                nc.scalar.activation(dst, src, COPY)
+        def round_w(pair):
+            dst = w_bf[pair].rearrange("p j m l -> p m l j")
+            src = w_raw.rearrange("p l (m j) -> p m l j", j=LANES)[:, :, :, 2 * pair:2 * pair + 2]
+            nc.scalar.activation(dst, src, COPY)
 
         def quant_w(j0, j1):
             cols = slice(j0 * P, j1 * P)
@@ -123,13 +123,9 @@ def tile_attend_gvq_pl_c_x_kernel(tc, zT, cb, wm, offs, out_0, out_1, out_2):
                                 start=True, stop=True)
             return acc
 
-        def drain(acc, first, j, a, b, on_vector=False):
+        def drain(acc, start, j, a, b):
             h = a // HALF
-            dst, src = y[h][:, j, a - h * HALF:b - h * HALF], acc[:, a - first:b - first]
-            if on_vector:
-                nc.vector.tensor_copy(dst, src)
-            else:
-                nc.scalar.activation(dst, src, COPY)
+            nc.scalar.activation(y[h][:, j, a - h * HALF:b - h * HALF], acc[:, a - start:b - start], COPY)
 
         def store_y(j0, j1, a, b):
             h = a // HALF
@@ -152,77 +148,73 @@ def tile_attend_gvq_pl_c_x_kernel(tc, zT, cb, wm, offs, out_0, out_1, out_2):
         def store_codes(a, b):
             nc.sync.dma_start(out=words_v[:, a:b], in_=y_codes[:, a:b].bitcast(I32))
 
-        def store_scales():
-            for k in range(4):
-                eng = nc.sync if k % 2 == 0 else nc.scalar
-                eng.dma_start(out=scales_v[4 * k:4 * k + 4, :], in_=y_scales[32 * k:32 * k + 4, :].bitcast(I32))
-
         nc.sync.dma_start(offsets[:], offs)
         for l in range(LANES):
-            load_book(l)
-            load_z_lane(l, 0, 512)
-        load_z(0, LANES, 512, 768)
+            nc.sync.dma_start(out=book[l][:, 0:C], in_=cb_v[:, l, :])
+            load_z_lane(l, 0, HALF)
+        load_z(0, LANES, HALF, Q3)
         nc.sync.dma_start(out=w_raw, in_=w_v)
-        load_z(0, 1, 768, T)
-        load_z(1, LANES, 768, T)
+        load_z(0, 1, Q3, T)
+        load_z(1, LANES, Q3, T)
         for l in range(3):
             nc.vector.memset(book[l][:, C:2 * C], 0.0)
 
-        nc.vector.tensor_copy(diff[768][:, 0, :], book[0][:].indirect(offsets[:, 48:64]))
+        nc.vector.tensor_copy(diff[Q3][:, 0, :], codewords(Q3, T, 0))
         for l in range(3):
-            gather(0, 512, l)
-        for a, b in ((0, 256), (256, 512)):
+            gather(0, HALF, l)
+        for a, b in ((0, Q1), (Q1, HALF)):
             gather(a, b, 3)
             round_g(a, b, False)
         for l in range(LANES):
-            gather(512, 768, l)
-        round_w(0, 0, 128, False)
-        round_w(1, 0, 128, False)
-        quant_g(0, 512)
-        nc.vector.tensor_tensor(diff[768][:, 0, :], diff[768][:, 0, :], z[0][768], SUB)
+            gather(HALF, Q3, l)
+        round_w(0)
+        round_w(1)
+        quant_g(0, HALF)
+        nc.vector.tensor_tensor(diff[Q3][:, 0, :], diff[Q3][:, 0, :], z[0][Q3], SUB)
         quant_w(0, 2)
-        gather(768, T, 1)
-        gather(768, T, 2)
-        gather(768, 896, 3)
+        gather(Q3, T, 1)
+        gather(Q3, T, 2)
         quant_w(2, 3)
+        gather(Q3, T, 3)
         quant_w(3, 4)
-        g_bf[512] = sb.tile([P, 256, LANES], BF16, name="g_bf512", tag="z768_0_1", align_bytes=64)
-        round_g(512, 768, False)
+        g_bf[HALF] = sb.tile([P, Q3 - HALF, LANES], BF16, name="g_bf512", tag="z768_0_1", align_bytes=64)
+        round_g(HALF, Q3, False)
         first = [multiply(j, 0, j) for j in range(LANES)]
-        gather(896, T, 3)
-        round_g(768, 896, True)
-        round_g(896, T, True)
-        quant_g(512, 768)
-        early = [multiply(j, 256, 4 + j) for j in range(2)]
-        quant_g(768, T)
+        round_g(Q3, T, True)
+        quant_g(HALF, Q3)
+        early = [multiply(j, Q1, LANES + j) for j in range(2)]
+        quant_g(Q3, T)
+
         for j in range(3):
-            drain(first[j], 0, j, 0, 512)
-            store_y(j, j + 1, 0, 512)
-        drain(first[3], 0, 3, 0, 256)
-        drain(first[3], 0, 3, 256, 512)
-        store_y(3, 4, 0, 512)
+            drain(first[j], 0, j, 0, HALF)
+            store_y(j, j + 1, 0, HALF)
+        drain(first[3], 0, 3, 0, Q1)
+        drain(first[3], 0, 3, Q1, HALF)
+        store_y(3, 4, 0, HALF)
         for j in range(2):
-            drain(early[j], 256, j, 512, 768)
-        store_y(0, 2, 512, 768)
-        last = {j: multiply(j, 512, bank) for j, bank in ((2, 6), (3, 7), (0, 0), (1, 1))}
-        round_y(0, 256, True)
-        round_y(256, 512, True)
-        quant_y(0, 256)
-        quant_y(256, 512)
-        drain(last[2], 512, 2, 512, T)
-        store_y(2, 3, 512, T)
+            drain(early[j], Q1, j, HALF, Q3)
+        store_y(0, 2, HALF, Q3)
+        last = {j: multiply(j, HALF, bank) for j, bank in ((2, 6), (3, 7), (0, 0), (1, 1))}
+        round_y(0, Q1, True)
+        round_y(Q1, HALF, True)
+        quant_y(0, Q1)
+        quant_y(Q1, HALF)
+        drain(last[2], HALF, 2, HALF, T)
+        store_y(2, 3, HALF, T)
         store_codes(0, HALF)
-        drain(last[3], 512, 3, 512, 768)
-        drain(last[3], 512, 3, 768, T)
-        store_y(3, 4, 512, T)
+        drain(last[3], HALF, 3, HALF, Q3)
+        drain(last[3], HALF, 3, Q3, T)
+        store_y(3, 4, HALF, T)
         for j in range(2):
-            drain(last[j], 512, j, 768, 1024, False)
-        store_y(0, 2, 768, 1024)
-        round_y(YM, 768, True)
-        round_y(512, YM, False)
-        round_y(768, YE, False)
-        round_y(YE, T, True)
-        quant_y(512, 768)
-        quant_y(768, T)
+            drain(last[j], HALF, j, Q3, T)
+        store_y(0, 2, Q3, T)
+        round_y(Y3_SPLIT, Q3, True)
+        round_y(HALF, Y3_SPLIT, False)
+        round_y(Q3, Y4_SPLIT, False)
+        round_y(Y4_SPLIT, T, True)
+        quant_y(HALF, Q3)
+        quant_y(Q3, T)
         store_codes(HALF, T)
-        store_scales()
+        for k in range(4):
+            queue = nc.sync if k % 2 == 0 else nc.scalar
+            queue.dma_start(out=scales_v[4 * k:4 * k + 4, :], in_=y_scales[32 * k:32 * k + 4, :].bitcast(I32))

@@ -107,7 +107,7 @@ def tile_attend_gvq_pl_c_x_kernel(tc, zT, cb, wm, offs, out_0, out_1, out_2):
         def round_w(pair):
             dst = w_bf[pair].rearrange("p j m l -> p m l j")
             src = w_raw.rearrange("p l (m j) -> p m l j", j=LANES)[:, :, :, 2 * pair:2 * pair + 2]
-            nc.scalar.activation(dst, src, COPY)
+            nc.scalar.copy(dst, src)
 
         def quant_w(j0, j1):
             cols = slice(j0 * P, j1 * P)
@@ -125,7 +125,7 @@ def tile_attend_gvq_pl_c_x_kernel(tc, zT, cb, wm, offs, out_0, out_1, out_2):
 
         def drain(acc, start, j, a, b):
             h = a // HALF
-            nc.scalar.activation(y[h][:, j, a - h * HALF:b - h * HALF], acc[:, a - start:b - start], COPY)
+            nc.scalar.copy(y[h][:, j, a - h * HALF:b - h * HALF], acc[:, a - start:b - start])
 
         def store_y(j0, j1, a, b):
             h = a // HALF
@@ -138,7 +138,7 @@ def tile_attend_gvq_pl_c_x_kernel(tc, zT, cb, wm, offs, out_0, out_1, out_2):
             if on_vector:
                 nc.vector.tensor_copy(dst, src)
             else:
-                nc.scalar.activation(dst, src, COPY)
+                nc.scalar.copy(dst, src)
 
         def quant_y(a, b):
             h = a // HALF

@@ -15,16 +15,15 @@ U8 = mybir.dt.uint8
 E4M3 = mybir.dt.float8_e4m3fn_x4
 E5M2 = mybir.dt.float8_e5m2_x4
 COPY = mybir.ActivationFunctionType.Copy
-SUB = mybir.AluOpType.subtract
+ADD = mybir.AluOpType.add
 MULT = mybir.AluOpType.mult
 
 P = 128
 LANES = 4
 Q1, HALF, Q3 = 256, 512, 768
 RUN = 4
-OVERLAP = 16
-Y3_SPLIT = 608
-Y4_SPLIT = 832
+WINDOW = (2048, 1024, 2048, 1024)
+Y_SPLIT = 896
 
 
 def weave(src, dst):
@@ -38,25 +37,22 @@ def tile_attend_gvq_pl_c_x_kernel(tc, zT, cb, wm, offs, out_0, out_1, out_2):
         ps = ctx.enter_context(tc.psum_pool(name="ps", bufs=1))
 
         offsets = sb.tile([P, T // 16], U16, name="offsets")
-        book = [sb.tile([P, 2 * C if l < 3 else C], F32, name="book%d" % l, tag="book%d" % l, align_bytes=64)
-                for l in range(LANES)]
-        z = [{} for l in range(LANES)]
-        w_at = LANES * (T - Q3) - OVERLAP
-        g_at = w_at + LANES * D - OVERLAP
-        late = sb.tile([P, g_at + LANES * (T - Q3) // 2], F32, name="late", align_bytes=64)
-        w_raw = late[:, w_at:w_at + LANES * D].rearrange("p (l d) -> p l d", l=LANES)
-        diff = {0: sb.tile([P, LANES, HALF], F32, name="diff0"),
-                HALF: sb.tile([P, LANES, Q3 - HALF], F32, name="diff512", tag="diff512"),
-                Q3: late[:, 0:LANES * (T - Q3)].rearrange("p (l t) -> p l t", l=LANES)}
-        g_bf = {0: sb.tile([P, HALF, LANES], BF16, name="g_bf0", align_bytes=64),
-                Q3: late[:, g_at:].bitcast(BF16).rearrange("p (t l) -> p t l", l=LANES)}
+        book = [sb.tile([P, WINDOW[l]], F32, name="book%d" % l, align_bytes=64) for l in range(LANES)]
+        first = sb.tile([P, LANES, HALF], F32, name="first", align_bytes=64)
+        second = sb.tile([P, LANES * HALF], F32, name="second", align_bytes=64)
+        picked = [first[:], second[:].rearrange("p (l t) -> p l t", l=LANES)]
+        z = {a: sb.tile([P, LANES, Q1], F32, name="z%d" % a, align_bytes=64)[:] for a in (Q1, HALF, Q3)}
+        z[0] = second[:, Q1:Q1 + LANES * Q1].rearrange("p (l t) -> p l t", l=LANES)
+        g_bf = sb.tile([P, T, LANES], BF16, name="g_bf", align_bytes=64)
         g_codes = sb.tile([P, T], U32, name="g_codes", align_bytes=64)
         g_scales = sb.tile([P, T], U8, name="g_scales", align_bytes=64)
-        w_bf = [sb.tile([P, 2, P, LANES], BF16, name="w_bf%d" % pair, align_bytes=64)[:] for pair in range(2)]
+        w_raw = sb.tile([P, LANES, D], F32, name="w_raw", align_bytes=64)
+        w_bf = [sb.tile([P, 2, P, LANES], BF16, name="w_bf%d" % pair, align_bytes=64) for pair in range(2)]
         w_codes = sb.tile([P, D], U32, name="w_codes", align_bytes=64)
         w_scales = sb.tile([P, D], U8, name="w_scales", align_bytes=64)
-        y = [sb.tile([P, LANES, HALF], F32, name="y%d" % h) for h in range(2)]
-        y_bf = [sb.tile([P, HALF, LANES], BF16, name="y_bf%d" % h, align_bytes=64) for h in range(2)]
+        pieces = ((0, HALF), (HALF, Q3), (Q3, T))
+        y = {a: sb.tile([P, LANES, b - a], F32, name="y%d" % a, align_bytes=64) for a, b in pieces}
+        y_bf = sb.tile([P, T, LANES], BF16, name="y_bf", align_bytes=64)
         y_codes = sb.tile([P, T], U32, name="y_codes", align_bytes=64)
         y_scales = sb.tile([P, T], U8, name="y_scales", align_bytes=64)
 
@@ -67,151 +63,125 @@ def tile_attend_gvq_pl_c_x_kernel(tc, zT, cb, wm, offs, out_0, out_1, out_2):
         words_v = out_1[0].rearrange("p t l -> p (t l)").bitcast(I32)
         scales_v = out_2[0].bitcast(I32)
 
-        def within(tiles, a, b):
-            start = max(s for s in tiles if s <= a)
-            return tiles[start], slice(a - start, b - start)
+        def y_at(a, b):
+            start = max(s for s in y if s <= a)
+            return y[start][:, :, a - start:b - start]
 
-        def load_z_lane(l, a, b):
-            tile = sb.tile([P, b - a], F32, name="z%d_%d" % (a, l))
-            nc.sync.dma_start(out=tile[:], in_=z_v[:, l, a:b])
-            z[l][a] = tile[:]
+        def load_z(a):
+            nc.sync.dma_start(out=z[a], in_=z_v[:, :, a:a + Q1])
 
-        def load_z(l0, l1, a, b):
-            tile = sb.tile([P, l1 - l0, b - a], F32, name="z%d_%d_%d" % (a, l0, l1), align_bytes=64)
-            nc.sync.dma_start(out=tile[:], in_=z_v[:, l0:l1, a:b])
-            for l in range(l0, l1):
-                z[l][a] = tile[:, l - l0, :]
+        def codewords(a, b):
+            h = a // HALF
+            return picked[h][:, :, a - h * HALF:b - h * HALF]
 
-        def codewords(a, b, l):
-            return book[l][:].indirect(offsets[:, a // 16:b // 16])
-
-        def gather(a, b, l):
-            src, zc = within(z[l], a, b)
-            dst, dc = within(diff, a, b)
-            nc.vector.tensor_tensor(dst[:, l, dc], codewords(a, b, l), src[:, zc], SUB)
-
-        def round_g(a, b, on_vector):
-            src, sc = within(diff, a, b)
-            dst, dc = within(g_bf, a, b)
-            dst, src = weave(src[:, :, sc], dst[:, dc, :])
+        def gather(l, a, b, on_vector):
+            src = book[l][:].indirect(offsets[:, a // 16:b // 16])
             if on_vector:
-                nc.vector.tensor_scalar(dst, src, -BETA, None, MULT)
+                nc.vector.tensor_scalar(codewords(a, b)[:, l, :], src, -BETA, 0.0, MULT, ADD)
             else:
-                nc.scalar.activation(dst, src, COPY, scale=-BETA)
+                nc.scalar.activation(codewords(a, b)[:, l, :], src, COPY, scale=-BETA)
+
+        def form_g(a):
+            nc.vector.scalar_tensor_tensor(g_bf[:, a:a + Q1, :], z[a].rearrange("p l t -> p t l"), BETA,
+                                           codewords(a, a + Q1).rearrange("p l t -> p t l"), MULT, ADD)
 
         def quant_g(a, b):
-            src, sc = within(g_bf, a, b)
             nc.vector.quantize_mx(out=g_codes[:, a:b].bitcast(E5M2), scales=g_scales[:, a:b],
-                                  in_=src[:, sc, :].rearrange("p t l -> p (t l)"))
+                                  in_=g_bf[:, a:b, :].rearrange("p t l -> p (t l)"))
 
-        def round_w(pair):
-            dst = w_bf[pair].rearrange("p j m l -> p m l j")
-            src = w_raw.rearrange("p l (m j) -> p m l j", j=LANES)[:, :, :, 2 * pair:2 * pair + 2]
-            nc.scalar.copy(dst, src)
+        def round_w(pair, on_vector):
+            dst = w_bf[pair][:].rearrange("p j m l -> p m l j")
+            src = w_raw[:].rearrange("p l (m j) -> p m l j", j=LANES)[:, :, :, 2 * pair:2 * pair + 2]
+            if on_vector:
+                nc.vector.tensor_copy(dst, src)
+            else:
+                nc.scalar.copy(dst, src)
 
-        def quant_w(j0, j1):
-            cols = slice(j0 * P, j1 * P)
-            src = w_bf[j0 // 2][:, j0 % 2:j0 % 2 + j1 - j0, :, :]
+        def quant_w(pair):
+            cols = slice(2 * pair * P, 2 * (pair + 1) * P)
             nc.vector.quantize_mx(out=w_codes[:, cols].bitcast(E4M3), scales=w_scales[:, cols],
-                                  in_=src.rearrange("p j m l -> p (j m l)"))
+                                  in_=w_bf[pair][:].rearrange("p j m l -> p (j m l)"))
 
-        def multiply(j, a, bank):
-            cols = slice(j * P, (j + 1) * P)
-            acc = ps.tile([P, HALF], F32, name="acc%d_%d" % (j, a), tag="bank%d" % bank)
-            nc.tensor.matmul_mx(out=acc[:], lhsT=w_codes[:, cols].bitcast(E4M3), lhsT_scale=w_scales[:, cols],
-                                rhs=g_codes[:, a:a + HALF].bitcast(E5M2), rhs_scale=g_scales[:, a:a + HALF],
-                                start=True, stop=True)
+        def multiply(j0, j1, a, b, bank):
+            acc = ps.tile([P, j1 - j0, b - a], F32, name="acc%d" % bank)
+            for j in range(j0, j1):
+                cols = slice(j * P, (j + 1) * P)
+                nc.tensor.matmul_mx(out=acc[:, j - j0, :], lhsT=w_codes[:, cols].bitcast(E4M3),
+                                    lhsT_scale=w_scales[:, cols], rhs=g_codes[:, a:b].bitcast(E5M2),
+                                    rhs_scale=g_scales[:, a:b], start=True, stop=True)
             return acc
 
-        def drain(acc, start, j, a, b):
-            h = a // HALF
-            nc.scalar.copy(y[h][:, j, a - h * HALF:b - h * HALF], acc[:, a - start:b - start])
-
-        def store_y(j0, j1, a, b):
-            h = a // HALF
-            nc.sync.dma_start(out=out_v[:, j0:j1, a:b], in_=y[h][:, j0:j1, a - h * HALF:b - h * HALF])
+        def drain(acc, j0, j1, a, b, on_vector):
+            dst = y_at(a, b)[:, j0:j1, :]
+            if on_vector:
+                nc.vector.tensor_copy(dst, acc[:])
+            else:
+                nc.scalar.copy(dst, acc[:])
+            nc.sync.dma_start(out=out_v[:, j0:j1, a:b], in_=dst)
 
         def round_y(a, b, on_vector):
-            h = a // HALF
-            cols = slice(a - h * HALF, b - h * HALF)
-            dst, src = weave(y[h][:, :, cols], y_bf[h][:, cols, :])
+            dst, src = weave(y_at(a, b), y_bf[:, a:b, :])
             if on_vector:
                 nc.vector.tensor_copy(dst, src)
             else:
                 nc.scalar.copy(dst, src)
 
         def quant_y(a, b):
-            h = a // HALF
             nc.vector.quantize_mx(out=y_codes[:, a:b].bitcast(E4M3), scales=y_scales[:, a:b],
-                                  in_=y_bf[h][:, a - h * HALF:b - h * HALF, :].rearrange("p t l -> p (t l)"))
+                                  in_=y_bf[:, a:b, :].rearrange("p t l -> p (t l)"))
 
         def store_codes(a, b):
             nc.sync.dma_start(out=words_v[:, a:b], in_=y_codes[:, a:b].bitcast(I32))
 
+        idle = sb.tile([P, 2], F32, name="idle")
+        nc.vector.memset(idle[:, 0:1], 0.0)
+        nc.scalar.activation(idle[:, 1:2], idle[:, 0:1], COPY, scale=-BETA)
+
         nc.sync.dma_start(offsets[:], offs)
         for l in range(LANES):
             nc.sync.dma_start(out=book[l][:, 0:C], in_=cb_v[:, l, :])
-            load_z_lane(l, 0, HALF)
-        load_z(0, LANES, HALF, Q3)
-        nc.sync.dma_start(out=w_raw, in_=w_v)
-        load_z(0, 1, Q3, T)
-        load_z(1, LANES, Q3, T)
-        for l in range(3):
-            nc.vector.memset(book[l][:, C:2 * C], 0.0)
+            (nc.vector if l < 2 else nc.gpsimd).memset(book[l][:, C:], 0.0)
+        load_z(0)
+        load_z(Q1)
+        nc.sync.dma_start(out=w_raw[:], in_=w_v)
+        load_z(HALF)
+        load_z(Q3)
 
-        nc.vector.tensor_copy(diff[Q3][:, 0, :], codewords(Q3, T, 0))
-        for l in range(3):
-            gather(0, HALF, l)
-        for a, b in ((0, Q1), (Q1, HALF)):
-            gather(a, b, 3)
-            round_g(a, b, False)
-        for l in range(LANES):
-            gather(HALF, Q3, l)
-        round_w(0)
-        round_w(1)
-        quant_g(0, HALF)
-        nc.vector.tensor_tensor(diff[Q3][:, 0, :], diff[Q3][:, 0, :], z[0][Q3], SUB)
-        quant_w(0, 2)
-        gather(Q3, T, 1)
-        gather(Q3, T, 2)
-        quant_w(2, 3)
-        gather(Q3, T, 3)
-        quant_w(3, 4)
-        g_bf[HALF] = sb.tile([P, Q3 - HALF, LANES], BF16, name="g_bf512", tag="z768_0_1", align_bytes=64)
-        round_g(HALF, Q3, False)
-        first = [multiply(j, 0, j) for j in range(LANES)]
-        round_g(Q3, T, True)
+        gather(0, 0, HALF, True)
+        gather(0, HALF, Q3, False)
+        gather(1, 0, HALF, False)
+        gather(2, 0, HALF, True)
+        gather(3, 0, Q1, False)
+        gather(3, Q1, HALF, False)
+        gather(3, HALF, T, False)
+        form_g(0)
+        gather(1, HALF, T, False)
+        gather(2, HALF, T, False)
+        gather(0, Q3, T, False)
+        form_g(Q1)
+        quant_g(0, Q1)
+        quant_g(Q1, HALF)
+        round_w(0, True)
+        round_w(1, True)
+        quant_w(0)
+        quant_w(1)
+        for j in range(LANES):
+            drain(multiply(j, j + 1, 0, HALF, j), j, j + 1, 0, HALF, False)
+        form_g(HALF)
+        form_g(Q3)
         quant_g(HALF, Q3)
-        early = [multiply(j, Q1, LANES + j) for j in range(2)]
         quant_g(Q3, T)
-
-        for j in range(3):
-            drain(first[j], 0, j, 0, HALF)
-            store_y(j, j + 1, 0, HALF)
-        drain(first[3], 0, 3, 0, Q1)
-        drain(first[3], 0, 3, Q1, HALF)
-        store_y(3, 4, 0, HALF)
-        for j in range(2):
-            drain(early[j], Q1, j, HALF, Q3)
-        store_y(0, 2, HALF, Q3)
-        last = {j: multiply(j, HALF, bank) for j, bank in ((2, 6), (3, 7), (0, 0), (1, 1))}
+        for k, (a, b) in enumerate(pieces[1:]):
+            for pair in range(2):
+                drain(multiply(2 * pair, 2 * pair + 2, a, b, LANES + 2 * k + pair), 2 * pair, 2 * pair + 2, a, b, False)
         round_y(0, Q1, True)
         round_y(Q1, HALF, True)
         quant_y(0, Q1)
         quant_y(Q1, HALF)
-        drain(last[2], HALF, 2, HALF, T)
-        store_y(2, 3, HALF, T)
         store_codes(0, HALF)
-        drain(last[3], HALF, 3, HALF, Q3)
-        drain(last[3], HALF, 3, Q3, T)
-        store_y(3, 4, HALF, T)
-        for j in range(2):
-            drain(last[j], HALF, j, Q3, T)
-        store_y(0, 2, Q3, T)
-        round_y(Y3_SPLIT, Q3, True)
-        round_y(HALF, Y3_SPLIT, False)
-        round_y(Q3, Y4_SPLIT, False)
-        round_y(Y4_SPLIT, T, True)
+        round_y(HALF, Q3, True)
+        round_y(Q3, Y_SPLIT, False)
+        round_y(Y_SPLIT, T, True)
         quant_y(HALF, Q3)
         quant_y(Q3, T)
         store_codes(HALF, T)

@@ -23,6 +23,7 @@ LANES = 4
 Q1, HALF, Q3 = 256, 512, 768
 RUN = 4
 WINDOW = (2048, 1024, 2048, 1024)
+Z_PITCH = Q1 + 9
 Y_SPLIT = 896
 
 
@@ -38,11 +39,11 @@ def tile_attend_gvq_pl_c_x_kernel(tc, zT, cb, wm, offs, out_0, out_1, out_2):
 
         offsets = sb.tile([P, T // 16], U16, name="offsets")
         book = [sb.tile([P, WINDOW[l]], F32, name="book%d" % l, align_bytes=64) for l in range(LANES)]
-        first = sb.tile([P, LANES, HALF], F32, name="first", align_bytes=64)
-        second = sb.tile([P, LANES * HALF], F32, name="second", align_bytes=64)
-        picked = [first[:], second[:].rearrange("p (l t) -> p l t", l=LANES)]
-        z = {a: sb.tile([P, LANES, Q1], F32, name="z%d" % a, align_bytes=64)[:] for a in (Q1, HALF, Q3)}
-        z[0] = second[:, Q1:Q1 + LANES * Q1].rearrange("p (l t) -> p l t", l=LANES)
+        first = sb.tile([P, LANES, HALF + 1], F32, name="first", align_bytes=64)
+        second = sb.tile([P, LANES * (HALF + 1)], F32, name="second", align_bytes=64)
+        picked = [first[:, :, 0:HALF], second[:].rearrange("p (l t) -> p l t", l=LANES)[:, :, 0:HALF]]
+        z = {a: sb.tile([P, LANES, Z_PITCH], F32, name="z%d" % a, align_bytes=64)[:, :, 0:Q1] for a in (Q1, HALF, Q3)}
+        z[0] = second[:, Q1 + 8:Q1 + 8 + LANES * Z_PITCH].rearrange("p (l t) -> p l t", l=LANES)[:, :, 0:Q1]
         g_bf = sb.tile([P, T, LANES], BF16, name="g_bf", align_bytes=64)
         g_codes = sb.tile([P, T], U32, name="g_codes", align_bytes=64)
         g_scales = sb.tile([P, T], U8, name="g_scales", align_bytes=64)

@@ -163,14 +163,16 @@ def tile_attend_gvq_pl_c_x_kernel(tc, zT, cb, wm, offs, out_0, out_1, out_2):
         quant_g(0, Q1)
         quant_g(Q1, HALF)
         round_w(0, True)
-        round_w(1, True)
+        round_w(1, False)
         quant_w(0)
-        quant_w(1)
-        for j in range(LANES):
+        for j in range(2):
             drain(multiply(j, j + 1, 0, HALF, j), j, j + 1, 0, HALF, False)
         form_g(HALF)
-        form_g(Q3)
+        quant_w(1)
         quant_g(HALF, Q3)
+        for j in range(2, LANES):
+            drain(multiply(j, j + 1, 0, HALF, j), j, j + 1, 0, HALF, False)
+        form_g(Q3)
         quant_g(Q3, T)
         for k, (a, b) in enumerate(pieces[1:]):
             for pair in range(2):

@@ -16,13 +16,14 @@ E4M3 = mybir.dt.float8_e4m3fn_x4
 E5M2 = mybir.dt.float8_e5m2_x4
 COPY = mybir.ActivationFunctionType.Copy
 ADD = mybir.AluOpType.add
+SUB = mybir.AluOpType.subtract
 MULT = mybir.AluOpType.mult
 
 P = 128
 LANES = 4
 Q1, HALF, Q3 = 256, 512, 768
 RUN = 4
-WINDOW = (2048, 1024, 2048, 1024)
+PITCH = HALF + 1
 Z_PITCH = Q1 + 9
 Y_SPLIT = 896
 
@@ -38,12 +39,12 @@ def tile_attend_gvq_pl_c_x_kernel(tc, zT, cb, wm, offs, out_0, out_1, out_2):
         ps = ctx.enter_context(tc.psum_pool(name="ps", bufs=1))
 
         offsets = sb.tile([P, T // 16], U16, name="offsets")
-        book = [sb.tile([P, WINDOW[l]], F32, name="book%d" % l, align_bytes=64) for l in range(LANES)]
-        first = sb.tile([P, LANES, HALF + 1], F32, name="first", align_bytes=64)
-        second = sb.tile([P, LANES * (HALF + 1)], F32, name="second", align_bytes=64)
-        picked = [first[:, :, 0:HALF], second[:].rearrange("p (l t) -> p l t", l=LANES)[:, :, 0:HALF]]
-        z = {a: sb.tile([P, LANES, Z_PITCH], F32, name="z%d" % a, align_bytes=64)[:, :, 0:Q1] for a in (Q1, HALF, Q3)}
-        z[0] = second[:, Q1 + 8:Q1 + 8 + LANES * Z_PITCH].rearrange("p (l t) -> p l t", l=LANES)[:, :, 0:Q1]
+        book = [sb.tile([P, 2 * C], F32, name="book%d" % l, align_bytes=64) for l in range(LANES)]
+        diff = sb.tile([P, LANES, HALF], F32, name="diff", align_bytes=64)
+        z_lane = {l: sb.tile([P, HALF], F32, name="z_lane%d" % l, align_bytes=64)[:] for l in range(LANES)}
+        second = sb.tile([P, LANES * PITCH], F32, name="second", align_bytes=64)
+        picked = second[:].rearrange("p (l t) -> p l t", l=LANES)[:, :, 0:HALF]
+        z = {a: sb.tile([P, LANES, Z_PITCH], F32, name="z%d" % a, align_bytes=64)[:, :, 0:Q1] for a in (HALF, Q3)}
         g_bf = sb.tile([P, T, LANES], BF16, name="g_bf", align_bytes=64)
         g_codes = sb.tile([P, T], U32, name="g_codes", align_bytes=64)
         g_scales = sb.tile([P, T], U8, name="g_scales", align_bytes=64)
@@ -68,23 +69,28 @@ def tile_attend_gvq_pl_c_x_kernel(tc, zT, cb, wm, offs, out_0, out_1, out_2):
             start = max(s for s in y if s <= a)
             return y[start][:, :, a - start:b - start]
 
-        def load_z(a):
-            nc.sync.dma_start(out=z[a], in_=z_v[:, :, a:a + Q1])
+        def load_book(l):
+            nc.sync.dma_start(out=book[l][:, 0:C], in_=cb_v[:, l, :])
 
-        def codewords(a, b):
-            h = a // HALF
-            return picked[h][:, :, a - h * HALF:b - h * HALF]
+        def load_z_lane(l):
+            nc.sync.dma_start(out=z_lane[l], in_=z_v[:, l, 0:HALF])
 
-        def gather(l, a, b, on_vector):
-            src = book[l][:].indirect(offsets[:, a // 16:b // 16])
-            if on_vector:
-                nc.vector.tensor_scalar(codewords(a, b)[:, l, :], src, -BETA, 0.0, MULT, ADD)
-            else:
-                nc.scalar.activation(codewords(a, b)[:, l, :], src, COPY, scale=-BETA)
+        def codewords(l, a, b):
+            return book[l][:].indirect(offsets[:, a // 16:b // 16])
+
+        def gather_minus_z(l, a, b):
+            nc.vector.tensor_tensor(diff[:, l, a:b], codewords(l, a, b), z_lane[l][:, a:b], SUB)
+
+        def round_g(a, b):
+            dst, src = weave(diff[:, :, a:b], g_bf[:, a:b, :])
+            nc.vector.tensor_scalar(dst, src, -BETA, None, MULT)
+
+        def gather_second(l):
+            nc.scalar.activation(picked[:, l, :], codewords(l, HALF, T), COPY, scale=-BETA)
 
         def form_g(a):
             nc.vector.scalar_tensor_tensor(g_bf[:, a:a + Q1, :], z[a].rearrange("p l t -> p t l"), BETA,
-                                           codewords(a, a + Q1).rearrange("p l t -> p t l"), MULT, ADD)
+                                           picked[:, :, a - HALF:a - HALF + Q1].rearrange("p l t -> p t l"), MULT, ADD)
 
         def quant_g(a, b):
             nc.vector.quantize_mx(out=g_codes[:, a:b].bitcast(E5M2), scales=g_scales[:, a:b],
@@ -140,30 +146,25 @@ def tile_attend_gvq_pl_c_x_kernel(tc, zT, cb, wm, offs, out_0, out_1, out_2):
 
         nc.sync.dma_start(offsets[:], offs)
         for l in range(LANES):
-            nc.sync.dma_start(out=book[l][:, 0:C], in_=cb_v[:, l, :])
+            load_book(l)
+            load_z_lane(l)
             (nc.vector if l < 2 else nc.gpsimd).memset(book[l][:, C:], 0.0)
-        load_z(0)
-        load_z(Q1)
         nc.sync.dma_start(out=w_raw[:], in_=w_v)
-        load_z(HALF)
-        load_z(Q3)
+        for a in (HALF, Q3):
+            nc.sync.dma_start(out=z[a], in_=z_v[:, :, a:a + Q1])
 
-        gather(0, 0, HALF, True)
-        gather(0, HALF, Q3, False)
-        gather(1, 0, HALF, False)
-        gather(2, 0, HALF, True)
-        gather(3, 0, Q1, False)
-        gather(3, Q1, HALF, False)
-        gather(3, HALF, T, False)
-        form_g(0)
-        gather(1, HALF, T, False)
-        gather(2, HALF, T, False)
-        gather(0, Q3, T, False)
-        form_g(Q1)
+        for l in range(LANES):
+            gather_second(l)
+        for l in range(3):
+            gather_minus_z(l, 0, HALF)
+        gather_minus_z(3, 0, Q1)
+        gather_minus_z(3, Q1, HALF)
+        round_g(0, Q1)
+        round_g(Q1, HALF)
         quant_g(0, Q1)
-        quant_g(Q1, HALF)
         round_w(0, True)
         round_w(1, False)
+        quant_g(Q1, HALF)
         quant_w(0)
         for j in range(2):
             drain(multiply(j, j + 1, 0, HALF, j), j, j + 1, 0, HALF, False)

@@ -49,7 +49,8 @@ def tile_attend_gvq_pl_c_x_kernel(tc, zT, cb, wm, offs, out_0, out_1, out_2):
         g_codes = sb.tile([P, T], U32, name="g_codes", align_bytes=64)
         g_scales = sb.tile([P, T], U8, name="g_scales", align_bytes=64)
         w_raw = sb.tile([P, LANES, D], F32, name="w_raw", align_bytes=64)
-        w_bf = [sb.tile([P, 2, P, LANES], BF16, name="w_bf%d" % pair, align_bytes=64) for pair in range(2)]
+        w_bf = [g_bf[:, HALF:Q3, :].rearrange("p (j m) l -> p j m l", j=2),
+                sb.tile([P, 2, P, LANES], BF16, name="w_bf1", align_bytes=64)[:]]
         w_codes = sb.tile([P, D], U32, name="w_codes", align_bytes=64)
         w_scales = sb.tile([P, D], U8, name="w_scales", align_bytes=64)
         pieces = ((0, HALF), (HALF, Q3), (Q3, T))
@@ -97,7 +98,7 @@ def tile_attend_gvq_pl_c_x_kernel(tc, zT, cb, wm, offs, out_0, out_1, out_2):
                                   in_=g_bf[:, a:b, :].rearrange("p t l -> p (t l)"))
 
         def round_w(pair, on_vector):
-            dst = w_bf[pair][:].rearrange("p j m l -> p m l j")
+            dst = w_bf[pair].rearrange("p j m l -> p m l j")
             src = w_raw[:].rearrange("p l (m j) -> p m l j", j=LANES)[:, :, :, 2 * pair:2 * pair + 2]
             if on_vector:
                 nc.vector.tensor_copy(dst, src)
@@ -107,7 +108,7 @@ def tile_attend_gvq_pl_c_x_kernel(tc, zT, cb, wm, offs, out_0, out_1, out_2):
         def quant_w(pair):
             cols = slice(2 * pair * P, 2 * (pair + 1) * P)
             nc.vector.quantize_mx(out=w_codes[:, cols].bitcast(E4M3), scales=w_scales[:, cols],
-                                  in_=w_bf[pair][:].rearrange("p j m l -> p (j m l)"))
+                                  in_=w_bf[pair].rearrange("p j m l -> p (j m l)"))
 
         def multiply(j0, j1, a, b, bank):
             acc = ps.tile([P, j1 - j0, b - a], F32, name="acc%d" % bank)
@@ -162,9 +163,9 @@ def tile_attend_gvq_pl_c_x_kernel(tc, zT, cb, wm, offs, out_0, out_1, out_2):
         round_g(0, Q1)
         round_g(Q1, HALF)
         quant_g(0, Q1)
-        round_w(0, True)
-        round_w(1, False)
         quant_g(Q1, HALF)
+        round_w(0, False)
+        round_w(1, False)
         quant_w(0)
         for j in range(2):
             drain(multiply(j, j + 1, 0, HALF, j), j, j + 1, 0, HALF, False)

@@ -25,6 +25,7 @@ Q1, HALF, Q3 = 256, 512, 768
 RUN = 4
 PITCH = HALF + 1
 Z_PITCH = Q1 + 9
+G_SPLIT = 896
 Y_SPLIT = 896
 
 
@@ -48,9 +49,8 @@ def tile_attend_gvq_pl_c_x_kernel(tc, zT, cb, wm, offs, out_0, out_1, out_2):
         g_bf = sb.tile([P, T, LANES], BF16, name="g_bf", align_bytes=64)
         g_codes = sb.tile([P, T], U32, name="g_codes", align_bytes=64)
         g_scales = sb.tile([P, T], U8, name="g_scales", align_bytes=64)
-        w_raw = sb.tile([P, LANES, D], F32, name="w_raw", align_bytes=64)
-        w_bf = [g_bf[:, HALF:Q3, :].rearrange("p (j m) l -> p j m l", j=2),
-                sb.tile([P, 2, P, LANES], BF16, name="w_bf1", align_bytes=64)[:]]
+        w_raw = [sb.tile([P, LANES, D // 2], F32, name="w_raw%d" % h, align_bytes=64) for h in range(2)]
+        w_bf = [sb.tile([P, 2, P, LANES], BF16, name="w_bf%d" % pair, align_bytes=64) for pair in range(2)]
         w_codes = sb.tile([P, D], U32, name="w_codes", align_bytes=64)
         w_scales = sb.tile([P, D], U8, name="w_scales", align_bytes=64)
         pieces = ((0, HALF), (HALF, Q3), (Q3, T))
@@ -89,17 +89,18 @@ def tile_attend_gvq_pl_c_x_kernel(tc, zT, cb, wm, offs, out_0, out_1, out_2):
         def gather_second(l):
             nc.scalar.activation(picked[:, l, :], codewords(l, HALF, T), COPY, scale=-BETA)
 
-        def form_g(a):
-            nc.vector.scalar_tensor_tensor(g_bf[:, a:a + Q1, :], z[a].rearrange("p l t -> p t l"), BETA,
-                                           picked[:, :, a - HALF:a - HALF + Q1].rearrange("p l t -> p t l"), MULT, ADD)
+        def form_g(a, b):
+            start = a - a % Q1
+            nc.vector.scalar_tensor_tensor(g_bf[:, a:b, :], z[start][:, :, a - start:b - start].rearrange("p l t -> p t l"),
+                                           BETA, picked[:, :, a - HALF:b - HALF].rearrange("p l t -> p t l"), MULT, ADD)
 
         def quant_g(a, b):
             nc.vector.quantize_mx(out=g_codes[:, a:b].bitcast(E5M2), scales=g_scales[:, a:b],
                                   in_=g_bf[:, a:b, :].rearrange("p t l -> p (t l)"))
 
-        def round_w(pair, on_vector):
-            dst = w_bf[pair].rearrange("p j m l -> p m l j")
-            src = w_raw[:].rearrange("p l (m j) -> p m l j", j=LANES)[:, :, :, 2 * pair:2 * pair + 2]
+        def round_w(h, pair, on_vector):
+            dst = w_bf[pair][:, :, h * P // 2:(h + 1) * P // 2, :].rearrange("p j m l -> p m l j")
+            src = w_raw[h][:].rearrange("p l (m j) -> p m l j", j=LANES)[:, :, :, 2 * pair:2 * pair + 2]
             if on_vector:
                 nc.vector.tensor_copy(dst, src)
             else:
@@ -108,7 +109,7 @@ def tile_attend_gvq_pl_c_x_kernel(tc, zT, cb, wm, offs, out_0, out_1, out_2):
         def quant_w(pair):
             cols = slice(2 * pair * P, 2 * (pair + 1) * P)
             nc.vector.quantize_mx(out=w_codes[:, cols].bitcast(E4M3), scales=w_scales[:, cols],
-                                  in_=w_bf[pair].rearrange("p j m l -> p (j m l)"))
+                                  in_=w_bf[pair][:].rearrange("p j m l -> p (j m l)"))
 
         def multiply(j0, j1, a, b, bank):
             acc = ps.tile([P, j1 - j0, b - a], F32, name="acc%d" % bank)
@@ -150,7 +151,8 @@ def tile_attend_gvq_pl_c_x_kernel(tc, zT, cb, wm, offs, out_0, out_1, out_2):
             load_book(l)
             load_z_lane(l)
             (nc.vector if l < 2 else nc.gpsimd).memset(book[l][:, C:], 0.0)
-        nc.sync.dma_start(out=w_raw[:], in_=w_v)
+        for h in range(2):
+            nc.sync.dma_start(out=w_raw[h][:], in_=w_v[:, :, h * D // 2:(h + 1) * D // 2])
         for a in (HALF, Q3):
             nc.sync.dma_start(out=z[a], in_=z_v[:, :, a:a + Q1])
 
@@ -164,17 +166,18 @@ def tile_attend_gvq_pl_c_x_kernel(tc, zT, cb, wm, offs, out_0, out_1, out_2):
         round_g(Q1, HALF)
         quant_g(0, Q1)
         quant_g(Q1, HALF)
-        round_w(0, False)
-        round_w(1, False)
+        round_w(0, 0, False)
+        round_w(0, 1, False)
+        round_w(1, 0, False)
+        round_w(1, 1, False)
         quant_w(0)
-        for j in range(2):
-            drain(multiply(j, j + 1, 0, HALF, j), j, j + 1, 0, HALF, False)
-        form_g(HALF)
         quant_w(1)
-        quant_g(HALF, Q3)
-        for j in range(2, LANES):
+        for j in range(LANES):
             drain(multiply(j, j + 1, 0, HALF, j), j, j + 1, 0, HALF, False)
-        form_g(Q3)
+        form_g(HALF, Q3)
+        form_g(Q3, G_SPLIT)
+        quant_g(HALF, Q3)
+        form_g(G_SPLIT, T)
         quant_g(Q3, T)
         for k, (a, b) in enumerate(pieces[1:]):
             for pair in range(2):

@@ -74,7 +74,7 @@ def tile_attend_gvq_pl_c_x_kernel(tc, zT, cb, wm, offs, out_0, out_1, out_2):
             nc.sync.dma_start(out=book[l][:, 0:C], in_=cb_v[:, l, :])
 
         def load_z_lane(l):
-            nc.sync.dma_start(out=z_lane[l], in_=z_v[:, l, 0:HALF])
+            (nc.scalar if l < 3 else nc.sync).dma_start(out=z_lane[l], in_=z_v[:, l, 0:HALF])
 
         def codewords(l, a, b):
             return book[l][:].indirect(offsets[:, a // 16:b // 16])
@@ -142,10 +142,6 @@ def tile_attend_gvq_pl_c_x_kernel(tc, zT, cb, wm, offs, out_0, out_1, out_2):
         def store_codes(a, b):
             nc.sync.dma_start(out=words_v[:, a:b], in_=y_codes[:, a:b].bitcast(I32))
 
-        idle = sb.tile([P, 2], F32, name="idle")
-        nc.vector.memset(idle[:, 0:1], 0.0)
-        nc.scalar.activation(idle[:, 1:2], idle[:, 0:1], COPY, scale=-BETA)
-
         nc.sync.dma_start(offsets[:], offs)
         for l in range(LANES):
             load_book(l)
@@ -155,6 +151,10 @@ def tile_attend_gvq_pl_c_x_kernel(tc, zT, cb, wm, offs, out_0, out_1, out_2):
             nc.sync.dma_start(out=w_raw[h][:], in_=w_v[:, :, h * D // 2:(h + 1) * D // 2])
         for a in (HALF, Q3):
             nc.sync.dma_start(out=z[a], in_=z_v[:, :, a:a + Q1])
+
+        idle = sb.tile([P, 2], F32, name="idle")
+        nc.vector.memset(idle[:, 0:1], 0.0)
+        nc.scalar.activation(idle[:, 1:2], idle[:, 0:1], COPY, scale=-BETA)
 
         for l in range(LANES):
             gather_second(l)

from contextlib import ExitStack

import concourse.mybir as mybir

T, C, D, DV = 1024, 512, 512, 512
BETA = 0.25
FLOPS = 2 * T * D * DV

F32 = mybir.dt.float32
BF16 = mybir.dt.bfloat16
I32 = mybir.dt.int32
U32 = mybir.dt.uint32
U16 = mybir.dt.uint16
U8 = mybir.dt.uint8
E4M3 = mybir.dt.float8_e4m3fn_x4
E5M2 = mybir.dt.float8_e5m2_x4
COPY = mybir.ActivationFunctionType.Copy
ADD = mybir.AluOpType.add
SUB = mybir.AluOpType.subtract
MULT = mybir.AluOpType.mult

P = 128
LANES = 4
Q1, HALF, Q3 = 256, 512, 768
RUN = 4
PITCH = HALF + 1
Z_PITCH = Q1 + 9
G_SPLIT = 896
Y_SPLIT = 896


def weave(src, dst):
    return (dst.rearrange("p (c i) l -> p c l i", i=RUN), src.rearrange("p l (c i) -> p c l i", i=RUN))


def tile_attend_gvq_pl_c_x_kernel(tc, zT, cb, wm, offs, out_0, out_1, out_2):
    nc = tc.nc
    with ExitStack() as ctx:
        sb = ctx.enter_context(tc.tile_pool(name="sb", bufs=1))
        ps = ctx.enter_context(tc.psum_pool(name="ps", bufs=1))

        offsets = sb.tile([P, T // 16], U16, name="offsets")
        book = [sb.tile([P, 2 * C], F32, name="book%d" % l, align_bytes=64) for l in range(LANES)]
        diff = sb.tile([P, LANES, HALF], F32, name="diff", align_bytes=64)
        z_lane = {l: sb.tile([P, HALF], F32, name="z_lane%d" % l, align_bytes=64)[:] for l in range(LANES)}
        second = sb.tile([P, LANES * PITCH], F32, name="second", align_bytes=64)
        picked = second[:].rearrange("p (l t) -> p l t", l=LANES)[:, :, 0:HALF]
        z = {a: sb.tile([P, LANES, Z_PITCH], F32, name="z%d" % a, align_bytes=64)[:, :, 0:Q1] for a in (HALF, Q3)}
        g_bf = sb.tile([P, T, LANES], BF16, name="g_bf", align_bytes=64)
        g_codes = sb.tile([P, T], U32, name="g_codes", align_bytes=64)
        g_scales = sb.tile([P, T], U8, name="g_scales", align_bytes=64)
        w_raw = [sb.tile([P, LANES, D // 2], F32, name="w_raw%d" % h, align_bytes=64) for h in range(2)]
        w_bf = [sb.tile([P, 2, P, LANES], BF16, name="w_bf%d" % pair, align_bytes=64) for pair in range(2)]
        w_codes = sb.tile([P, D], U32, name="w_codes", align_bytes=64)
        w_scales = sb.tile([P, D], U8, name="w_scales", align_bytes=64)
        pieces = ((0, HALF), (HALF, Q3), (Q3, T))
        y = {a: sb.tile([P, LANES, b - a], F32, name="y%d" % a, align_bytes=64) for a, b in pieces}
        y_bf = sb.tile([P, T, LANES], BF16, name="y_bf", align_bytes=64)
        y_codes = sb.tile([P, T], U32, name="y_codes", align_bytes=64)
        y_scales = sb.tile([P, T], U8, name="y_scales", align_bytes=64)

        cb_v = cb.rearrange("(p l) c -> p l c", l=LANES)
        z_v = zT.rearrange("(p l) t -> p l t", l=LANES)
        w_v = wm.rearrange("(p l) d -> p l d", l=LANES)
        out_v = out_0.rearrange("(p l) t -> p l t", l=LANES)
        words_v = out_1[0].rearrange("p t l -> p (t l)").bitcast(I32)
        scales_v = out_2[0].bitcast(I32)

        def y_at(a, b):
            start = max(s for s in y if s <= a)
            return y[start][:, :, a - start:b - start]

        def load_book(l):
            nc.sync.dma_start(out=book[l][:, 0:C], in_=cb_v[:, l, :])

        def load_z_lane(l):
            (nc.scalar if l < 3 else nc.sync).dma_start(out=z_lane[l], in_=z_v[:, l, 0:HALF])

        def codewords(l, a, b):
            return book[l][:].indirect(offsets[:, a // 16:b // 16])

        def gather_minus_z(l, a, b):
            nc.vector.tensor_tensor(diff[:, l, a:b], codewords(l, a, b), z_lane[l][:, a:b], SUB)

        def round_g(a, b):
            dst, src = weave(diff[:, :, a:b], g_bf[:, a:b, :])
            nc.vector.tensor_scalar(dst, src, -BETA, None, MULT)

        def gather_second(l):
            nc.scalar.activation(picked[:, l, :], codewords(l, HALF, T), COPY, scale=-BETA)

        def form_g(a, b):
            start = a - a % Q1
            nc.vector.scalar_tensor_tensor(g_bf[:, a:b, :], z[start][:, :, a - start:b - start].rearrange("p l t -> p t l"),
                                           BETA, picked[:, :, a - HALF:b - HALF].rearrange("p l t -> p t l"), MULT, ADD)

        def quant_g(a, b):
            nc.vector.quantize_mx(out=g_codes[:, a:b].bitcast(E5M2), scales=g_scales[:, a:b],
                                  in_=g_bf[:, a:b, :].rearrange("p t l -> p (t l)"))

        def round_w(h, pair, on_vector):
            dst = w_bf[pair][:, :, h * P // 2:(h + 1) * P // 2, :].rearrange("p j m l -> p m l j")
            src = w_raw[h][:].rearrange("p l (m j) -> p m l j", j=LANES)[:, :, :, 2 * pair:2 * pair + 2]
            if on_vector:
                nc.vector.tensor_copy(dst, src)
            else:
                nc.scalar.copy(dst, src)

        def quant_w(pair):
            cols = slice(2 * pair * P, 2 * (pair + 1) * P)
            nc.vector.quantize_mx(out=w_codes[:, cols].bitcast(E4M3), scales=w_scales[:, cols],
                                  in_=w_bf[pair][:].rearrange("p j m l -> p (j m l)"))

        def multiply(j0, j1, a, b, bank):
            acc = ps.tile([P, j1 - j0, b - a], F32, name="acc%d" % bank)
            for j in range(j0, j1):
                cols = slice(j * P, (j + 1) * P)
                nc.tensor.matmul_mx(out=acc[:, j - j0, :], lhsT=w_codes[:, cols].bitcast(E4M3),
                                    lhsT_scale=w_scales[:, cols], rhs=g_codes[:, a:b].bitcast(E5M2),
                                    rhs_scale=g_scales[:, a:b], start=True, stop=True)
            return acc

        def drain(acc, j0, j1, a, b, on_vector):
            dst = y_at(a, b)[:, j0:j1, :]
            if on_vector:
                nc.vector.tensor_copy(dst, acc[:])
            else:
                nc.scalar.copy(dst, acc[:])
            nc.sync.dma_start(out=out_v[:, j0:j1, a:b], in_=dst)

        def round_y(a, b, on_vector):
            dst, src = weave(y_at(a, b), y_bf[:, a:b, :])
            if on_vector:
                nc.vector.tensor_copy(dst, src)
            else:
                nc.scalar.copy(dst, src)

        def quant_y(a, b):
            nc.vector.quantize_mx(out=y_codes[:, a:b].bitcast(E4M3), scales=y_scales[:, a:b],
                                  in_=y_bf[:, a:b, :].rearrange("p t l -> p (t l)"))

        def store_codes(a, b):
            nc.sync.dma_start(out=words_v[:, a:b], in_=y_codes[:, a:b].bitcast(I32))

        nc.sync.dma_start(offsets[:], offs)
        for l in range(LANES):
            load_book(l)
            load_z_lane(l)
            (nc.vector if l < 2 else nc.gpsimd).memset(book[l][:, C:], 0.0)
        for h in range(2):
            nc.sync.dma_start(out=w_raw[h][:], in_=w_v[:, :, h * D // 2:(h + 1) * D // 2])
        for a in (HALF, Q3):
            nc.sync.dma_start(out=z[a], in_=z_v[:, :, a:a + Q1])

        idle = sb.tile([P, 2], F32, name="idle")
        nc.vector.memset(idle[:, 0:1], 0.0)
        nc.scalar.activation(idle[:, 1:2], idle[:, 0:1], COPY, scale=-BETA)

        for l in range(LANES):
            gather_second(l)
        for l in range(3):
            gather_minus_z(l, 0, HALF)
        gather_minus_z(3, 0, Q1)
        gather_minus_z(3, Q1, HALF)
        round_g(0, Q1)
        round_g(Q1, HALF)
        quant_g(0, Q1)
        quant_g(Q1, HALF)
        round_w(0, 0, False)
        round_w(0, 1, False)
        round_w(1, 0, False)
        round_w(1, 1, False)
        quant_w(0)
        quant_w(1)
        for j in range(LANES):
            drain(multiply(j, j + 1, 0, HALF, j), j, j + 1, 0, HALF, False)
        form_g(HALF, Q3)
        form_g(Q3, G_SPLIT)
        quant_g(HALF, Q3)
        form_g(G_SPLIT, T)
        quant_g(Q3, T)
        for k, (a, b) in enumerate(pieces[1:]):
            for pair in range(2):
                drain(multiply(2 * pair, 2 * pair + 2, a, b, LANES + 2 * k + pair), 2 * pair, 2 * pair + 2, a, b, False)
        round_y(0, Q1, True)
        round_y(Q1, HALF, True)
        quant_y(0, Q1)
        quant_y(Q1, HALF)
        store_codes(0, HALF)
        round_y(HALF, Q3, True)
        round_y(Q3, Y_SPLIT, False)
        round_y(Y_SPLIT, T, True)
        quant_y(HALF, Q3)
        quant_y(Q3, T)
        store_codes(HALF, T)
        for k in range(4):
            queue = nc.sync if k % 2 == 0 else nc.scalar
            queue.dma_start(out=scales_v[4 * k:4 * k + 4, :], in_=y_scales[32 * k:32 * k + 4, :].bitcast(I32))
